import numpy as np
import ml_dtypes


def mxq(x, axis, fmt="e4m3"):
    dtype, down = {"e4m3": (ml_dtypes.float8_e4m3fn, 7), "e5m2": (ml_dtypes.float8_e5m2, 14)}[fmt]
    v = np.moveaxis(np.asarray(x, np.float32).astype(ml_dtypes.bfloat16).astype(np.float64), axis, -1)
    blocks = v.reshape(v.shape[:-1] + (-1, 32))
    amax = np.abs(blocks).max(-1, keepdims=True)
    byte = np.maximum(np.where(amax > 0, np.frexp(amax)[1] - 1 + 127, 0) - down, 1)
    scale = np.exp2(byte - 127.0)
    codes = (blocks / scale).astype(np.float32).astype(dtype).astype(np.float64)
    return np.moveaxis((codes * scale).reshape(v.shape), -1, axis)


WIDE = False


def mx_kscale(k):
    if not WIDE:
        return np.ones(k)
    levels = np.array([10, -10, 5, -5, 0])
    if k % 512:
        return np.exp2(np.random.permutation(np.resize(levels, k // 32))).repeat(32)
    a = np.empty((k // 512, 16))
    for p in range(k // 512):
        a[p, :8] = np.random.permutation(np.resize(levels, 8))
        for g in range(8):
            far = levels[np.abs(levels - a[p, g]) >= 10]
            a[p, g + 8] = far[np.random.randint(len(far))]
    return np.exp2(a.ravel()).repeat(32)


def f64(x):
    return np.asarray(x).astype(np.float64)


def striped(idx):
    return np.tile(idx.reshape(-1, 16).T, (8, 1)).astype(np.uint16)


def unstriped(offs):
    return offs[:16].T.reshape(-1).astype(np.int64)


E2M1 = np.array([0.0, 0.5, 1.0, 1.5, 2.0, 3.0, 4.0, 6.0, -0.0, -0.5, -1.0, -1.5, -2.0, -3.0, -4.0, -6.0])


def pack_weight(w, fmt):
    k, n = w.shape
    w = f64(np.asarray(w, np.float32).astype(ml_dtypes.bfloat16)).reshape(k // 32, 32, n)
    amax = np.abs(w).max(1)
    if fmt == "e4m3":
        byte = np.frexp(amax)[1] - 1 + 127 - 7
    else:
        mant, ex = np.frexp(amax / 6.0)
        byte = np.where(mant > 0.5, ex, ex - 1) + 127
    byte = np.clip(np.where(amax > 0, byte, 1), 1, 254)
    scaled = (w * np.exp2(127.0 - byte)[:, None, :]).reshape(k, n).astype(np.float32)
    by_word = np.ascontiguousarray(scaled.reshape(k // 512, 128, 4, n).transpose(0, 1, 3, 2))
    if fmt == "e4m3":
        words = by_word.astype(ml_dtypes.float8_e4m3fn).view(np.uint8)
    else:
        c = by_word.astype(ml_dtypes.float4_e2m1fn).view(np.uint8) & 0xF
        words = (c[..., 0::2] | (c[..., 1::2] << 4)).reshape(k // 512, 128, 2 * n)
    return np.ascontiguousarray(words), np.ascontiguousarray(byte.astype(np.uint8).reshape(k // 512, 16, n))


def unpack_weight(words, scales, fmt):
    g, _, n = scales.shape
    words = np.ascontiguousarray(words).reshape(g, 128, n, -1)
    if fmt == "e4m3":
        vals = words.view(ml_dtypes.float8_e4m3fn).astype(np.float64)
    else:
        nib = np.empty((g, 128, n, 4), np.uint8)
        nib[..., 0::2] = words & 0xF
        nib[..., 1::2] = words >> 4
        vals = E2M1[nib]
    vals = vals * np.repeat(np.exp2(scales.astype(np.float64) - 127.0), 8, axis=1)[..., None]
    return vals.transpose(0, 1, 3, 2).reshape(g * 512, n)


def gelu(v):
    return 0.5 * v * (1.0 + np.tanh(np.sqrt(2.0 / np.pi) * (v + 0.044715 * v**3)))


K, H, T, S, T2, P = 1536, 512, 4096, 1024, 2048, 1024


def setup_inputs():
    n = np.random.standard_normal
    s = mx_kscale(K)[:, None]
    u = mx_kscale(H)[:, None]
    d = {}
    d["tab_words"], d["tab_scales"] = pack_weight(n((K, T)) * s, "e4m3")
    d["offs"] = striped(np.random.permutation(T)[:S])
    d["offs2"] = striped(np.random.permutation(T2)[:S])
    d["offs3"] = striped(np.random.permutation(T2)[:P])
    d["offs4"] = striped(np.random.permutation(T2)[:P])
    d["wa"] = (1.3 * n((K, H)) / s / K ** 0.5).astype(np.float32)
    d["wb_words"], d["wb_scales"] = pack_weight(n((K, H)) / s / K ** 0.5, "e2m1")
    d["gain"] = (np.exp(0.3 * n(H)) * u[:, 0]).astype(np.float32)
    d["wgs"] = np.exp(0.3 * n((128, S))).astype(np.float32)
    d["page0"] = (n((H, T2)) * u).astype(np.float32)
    d["sx"] = np.exp(0.3 * n(H)).astype(np.float32)
    d["wr"] = (1.3 * n((H, H)) / u / H ** 0.5).astype(np.float32)
    d["sv"] = (np.exp(0.3 * n(H)) / u[:, 0]).astype(np.float32)
    return d


def reference(tab_words, tab_scales, offs, offs2, offs3, offs4, wa, wb_words, wb_scales,
              gain, wgs, page0, sx, wr, sv):
    v = unpack_weight(tab_words, tab_scales, "e4m3")[:, unstriped(offs)]
    warm = mxq(f64(wa), 0, "e4m3").T @ v
    wear = unpack_weight(wb_words, wb_scales, "e2m1").T @ v
    h = (np.tanh(warm) - np.abs(wear)) * f64(gain)[:, None]
    page = f64(page0).copy()
    page[:, unstriped(offs2)] = np.tile(f64(wgs), (H // 128, 1)) * h
    x = page[:, unstriped(offs3)] * f64(sx)[:, None]
    y = mxq(f64(wr), 0, "e4m3").T @ mxq(x, 0, "e4m3")
    sister = page[:, unstriped(offs4)] * f64(sv)[:, None]
    return np.minimum(y, sister) + sister

@@ -1,0 +1,307 @@
+from contextlib import ExitStack
+
+import concourse.mybir as mybir
+from concourse.masks import make_identity
+
+K, H, T, S, T2, NP = 1536, 512, 4096, 1024, 2048, 1024
+FLOPS = 2 * K * H * S * 2 + 2 * H * H * NP
+
+F32 = mybir.dt.float32
+BF16 = mybir.dt.bfloat16
+I32 = mybir.dt.int32
+U32 = mybir.dt.uint32
+U16 = mybir.dt.uint16
+U8 = mybir.dt.uint8
+FP8X4 = mybir.dt.float8_e4m3fn_x4
+FP4X4 = mybir.dt.float4_e2m1fn_x4
+ALU = mybir.AluOpType
+ACT = mybir.ActivationFunctionType
+
+P = 128
+PASSES = K // 512
+TILES = H // P
+HALF = 512
+SUB = HALF // P
+
+
+def tile_list_swab_cavity_scores_kernel(
+    tc, tab_words, tab_scales, offs, offs2, offs3, offs4, wa, wb_words, wb_scales,
+    gain, wgs, page0, sx, wr, sv, out,
+):
+    nc = tc.nc
+    with ExitStack() as ctx:
+        keep = ctx.enter_context(tc.tile_pool(name="keep", bufs=1))
+        ring = ctx.enter_context(tc.tile_pool(name="ring", bufs=2))
+        psum = ctx.enter_context(tc.psum_pool(name="psum", bufs=4))
+
+        def load_list(name, src):
+            lst = keep.tile([P, S // 16], U16, name=name)
+            nc.sync.dma_start(lst[:], src)
+            return lst
+
+        def load_column_vector(name, src):
+            cols = keep.tile([P, TILES], F32, name=name)
+            with nc.allow_non_contiguous_dma(reason="one value a partition"):
+                nc.sync.dma_start(cols[:], src.rearrange("(t p) -> p t", p=P))
+            return cols
+
+        def load_table(a):
+            tab = keep.tile([P, T], I32, name="tab%d" % a)
+            nc.sync.dma_start(tab[:], tab_words[a].rearrange("p t i -> p (t i)").bitcast(I32))
+            return tab
+
+        def load_wa(t):
+            raw = keep.tile([P, 2048], F32, name="wa_raw%d" % t)
+            for a in range(PASSES):
+                nc.sync.dma_start(
+                    raw[:, 512 * a : 512 * (a + 1)].rearrange("p (j c) -> p j c", j=4),
+                    wa[512 * a : 512 * (a + 1), P * t : P * (t + 1)].rearrange("(p j) c -> p j c", j=4),
+                )
+            return raw
+
+        def load_page(t):
+            page = keep.tile([P, T2], F32, name="page%d" % t)
+            nc.sync.dma_start(page[:], page0[P * t : P * (t + 1), :])
+            return page
+
+        scale_win = keep.tile([P, T], U8, name="scale_win")
+        nc.vector.memset(scale_win[:].bitcast(I32), 0)
+        for q in range(4):
+            nc.gpsimd.dma_start(
+                scale_win[32 * q : 32 * q + 4 * PASSES, :].bitcast(I32),
+                tab_scales[:, 4 * q : 4 * q + 4, :].bitcast(I32),
+            )
+        wb_planes = keep.tile([P, PASSES, H], U8, name="wb_planes", align_bytes=64)
+        nc.vector.memset(wb_planes[:].bitcast(I32), 0)
+        for q in range(4):
+            nc.gpsimd.dma_start(
+                wb_planes[32 * q : 32 * q + 4, :, :].bitcast(I32),
+                wb_scales[:, 4 * q : 4 * q + 4, :].rearrange("a r n -> r a n").bitcast(I32),
+            )
+        picked_scales = keep.tile([P, S], U8, name="picked_scales", align_bytes=64)
+        tab_planes = [picked_scales]
+        for a in range(1, PASSES):
+            plane = keep.tile([P, S], U8, name="tab_plane%d" % a, align_bytes=64)
+            nc.vector.memset(plane[:].bitcast(I32), 0)
+            tab_planes.append(plane)
+
+        idx = load_list("idx", offs)
+        gain_cols = load_column_vector("gain_cols", gain)
+        tabs = [load_table(0)]
+        wa_raw = [load_wa(0)]
+        wb_codes = keep.tile([P, PASSES, 2 * H], U8, name="wb_codes", align_bytes=64)
+        nc.sync.dma_start(wb_codes[:].bitcast(I32), wb_words.rearrange("a p n -> p a n").bitcast(I32))
+        tabs.append(load_table(1))
+        tabs.append(load_table(2))
+        idx2 = load_list("idx2", offs2)
+        pages = [load_page(0)]
+        wgs_sb = keep.tile([P, S], F32, name="wgs_sb")
+        for h in range(2):
+            nc.sync.dma_start(wgs_sb[:, HALF * h : HALF * (h + 1)], wgs[:, HALF * h : HALF * (h + 1)])
+        idx3 = load_list("idx3", offs3)
+        sx_cols = load_column_vector("sx_cols", sx)
+        wa_raw.append(load_wa(1))
+        idx4 = load_list("idx4", offs4)
+        sv_cols = load_column_vector("sv_cols", sv)
+        wa_raw.append(load_wa(2))
+        pages.append(load_page(1))
+        wa_raw.append(load_wa(3))
+        pages.append(load_page(2))
+        wr_raw = keep.tile([P, 4, H], F32, name="wr_raw")
+        nc.sync.dma_start(wr_raw[:], wr.rearrange("(p j) n -> p j n", j=4))
+        pages.append(load_page(3))
+
+        ident32 = keep.tile([P, P], F32, name="ident32")
+        make_identity(nc, ident32[:])
+        ident16 = keep.tile([P, P], BF16, name="ident16")
+        make_identity(nc, ident16[:])
+        neg_gain = keep.tile([P, TILES], F32, name="neg_gain")
+        nc.vector.tensor_scalar(neg_gain[:], gain_cols[:], -1.0, None, ALU.mult)
+
+        nc.vector.tensor_copy(picked_scales[:], scale_win[:].indirect(idx[:]))
+        for a in range(1, PASSES):
+            nc.gpsimd.dma_start(
+                tab_planes[a][0:100, :].bitcast(I32), picked_scales[4 * a : 4 * a + 100, :].bitcast(I32)
+            )
+        picked = {}
+        for a in range(PASSES):
+            words = keep.tile([P, S], U32, name="picked%d" % a, align_bytes=64)
+            for h in range(2):
+                half = words[:, HALF * h : HALF * (h + 1)]
+                nc.vector.tensor_copy(half, tabs[a][:].bitcast(U32).indirect(idx[:, 32 * h : 32 * (h + 1)]))
+                picked[a, h] = half
+
+        LEFT = 256
+        boards = [keep.tile([P, LEFT + S + HALF], F32, name="board%d" % i, align_bytes=64) for i in range(2)]
+        first_staging = keep.tile([P, PASSES * 512], BF16, name="first_staging", align_bytes=64)
+
+        def staging(n, width):
+            if n == 0:
+                return first_staging[:]
+            board = boards[(n - 1) // 2]
+            words = width // 2
+            if n % 2 == 1:
+                return board[:, LEFT + HALF - words : LEFT + HALF].bitcast(BF16)
+            return board[:, LEFT + HALF : LEFT + HALF + words].bitcast(BF16)
+
+        def quantize_wa(t):
+            grouped = staging(t, PASSES * 512)
+            nc.scalar.copy(
+                grouped.rearrange("p (a c i j) -> p a c j i", a=PASSES, i=4, j=4),
+                wa_raw[t][:, 0 : PASSES * 512].rearrange("p (a j c i) -> p a c j i", a=PASSES, i=4, j=4),
+            )
+            codes = keep.tile([P, PASSES * P], U32, name="wa_codes%d" % t, align_bytes=64)
+            planes = keep.tile([P, PASSES * P], U8, name="wa_planes%d" % t, align_bytes=64)
+            for a in range(PASSES):
+                nc.vector.quantize_mx(
+                    out=codes[:, P * a : P * (a + 1)].bitcast(FP8X4),
+                    scales=planes[:, P * a : P * (a + 1)],
+                    in_=grouped[:, 512 * a : 512 * (a + 1)],
+                )
+            return codes, planes
+
+        def quantize_wr():
+            grouped = staging(TILES, 4 * H)
+            nc.scalar.copy(
+                grouped.rearrange("p (c i j) -> p c j i", i=4, j=4),
+                wr_raw[:].rearrange("p j (c i) -> p c j i", i=4),
+            )
+            codes = keep.tile([P, H], U32, name="wr_codes", align_bytes=64)
+            plane = keep.tile([P, H], U8, name="wr_plane", align_bytes=64)
+            nc.vector.quantize_mx(out=codes[:].bitcast(FP8X4), scales=plane[:], in_=grouped)
+            return codes, plane
+
+        def first_stage(t, wa_codes, wa_planes):
+            entries = boards[t % 2][:, LEFT : LEFT + S]
+            for h in range(2):
+                warm = psum.tile([P, HALF], F32, name="warm", tag="mx")
+                wear = psum.tile([P, HALF], F32, name="wear", tag="mx")
+                for a in range(PASSES):
+                    for b in range(SUB):
+                        first = a == 0 and b == 0
+                        last = a == PASSES - 1 and b == SUB - 1
+                        lhs = picked[a, h][:, P * b : P * (b + 1)].bitcast(FP8X4)
+                        lhs_scale = tab_planes[a][:, HALF * h + P * b : HALF * h + P * (b + 1)]
+                        nc.tensor.matmul_mx(
+                            out=warm[:, P * b : P * (b + 1)], lhsT=lhs, lhsT_scale=lhs_scale,
+                            rhs=wa_codes[:, P * a : P * (a + 1)].bitcast(FP8X4),
+                            rhs_scale=wa_planes[:, P * a : P * (a + 1)],
+                            start=first, stop=last,
+                        )
+                        nc.tensor.matmul_mx(
+                            out=wear[:, P * b : P * (b + 1)], lhsT=lhs, lhsT_scale=lhs_scale,
+                            rhs=wb_codes[:, a, 2 * P * t : 2 * P * (t + 1)].bitcast(FP4X4),
+                            rhs_scale=wb_planes[:, a, P * t : P * (t + 1)],
+                            start=first, stop=last,
+                        )
+                neg_tanh = ring.tile([P, HALF], F32, name="neg_tanh")
+                nc.scalar.activation(neg_tanh[:], warm[:], ACT.Tanh, scale=-1.0)
+                magnitude = ring.tile([P, HALF], F32, name="magnitude", bufs=3)
+                nc.scalar.activation(magnitude[:], wear[:], ACT.Abs)
+                turned = psum.tile([P, HALF], F32, name="turned", tag="tr")
+                for b in range(SUB):
+                    cols = slice(P * b, P * (b + 1))
+                    nc.tensor.matmul(turned[:, cols], neg_tanh[:, cols], ident32[:], start=True, stop=False, is_transpose=True)
+                    nc.tensor.matmul(turned[:, cols], magnitude[:, cols], ident32[:], start=False, stop=True, is_transpose=True)
+                nc.scalar.activation(
+                    entries[:, HALF * h : HALF * (h + 1)], turned[:], ACT.Copy, scale=neg_gain[:, t : t + 1]
+                )
+            return entries, magnitude
+
+        x_turned = [keep.tile([P, SUB, 2, P], F32, name="x_turned%d" % h) for h in range(2)]
+        sisters = {}
+
+        def gather_sister(t, dst):
+            nc.vector.tensor_copy(dst, pages[t][:].indirect(idx4[:]))
+            sisters[t] = dst
+
+        def put(t, h, entries):
+            cols = slice(HALF * h, HALF * (h + 1))
+            nc.vector.tensor_tensor(
+                pages[t][:].indirect(idx2[:, 32 * h : 32 * (h + 1)]), entries[:, cols], wgs_sb[:, cols], ALU.mult
+            )
+
+        def turn_x(t, spare, due):
+            for h in range(2):
+                x_rows = spare[:, 256 * h : 256 * (h + 1)].bitcast(BF16)
+                nc.scalar.activation(x_rows, due[:, HALF * h : HALF * (h + 1)], ACT.Copy, scale=sx_cols[:, t : t + 1])
+                x_cols = psum.tile([P, SUB, P], BF16, name="x_cols", tag="tr")
+                for b in range(SUB):
+                    nc.tensor.transpose(x_cols[:, b, :], x_rows[:, P * b : P * (b + 1)], ident16[:])
+                nc.scalar.copy(
+                    x_turned[h][:, :, :, 32 * t : 32 * (t + 1)],
+                    x_cols[:].bitcast(F32).rearrange("p b (q u) -> p b u q", u=2),
+                )
+
+        quantized = [quantize_wa(0)]
+        entries, spare = first_stage(0, *quantized[0])
+        for t in range(TILES):
+            for h in range(2):
+                put(t, h, entries)
+                n = 2 * t + h + 1
+                if n < TILES:
+                    quantized.append(quantize_wa(n))
+                elif n == TILES:
+                    wr_codes, wr_plane = quantize_wr()
+            due = wa_raw[(t + 1) % TILES][:, 0:NP]
+            get_pieces = 2 if t == TILES - 1 else 1
+            for i in range(get_pieces):
+                n = NP // get_pieces
+                nc.vector.tensor_copy(
+                    due[:, i * n : (i + 1) * n], pages[t][:].indirect(idx3[:, i * n // 16 : (i + 1) * n // 16])
+                )
+            if t == 0:
+                gather_sister(0, wa_raw[1][:, NP : 2 * NP])
+            if t + 1 < TILES:
+                entries, spare = first_stage(t + 1, *quantized[t + 1])
+            turn_x(t, spare, due)
+        gather_sister(1, wgs_sb[:])
+        gather_sister(2, entries)
+
+        x_grouped, x_codes, x_planes = [], [], []
+        for h in range(2):
+            grouped = keep.tile([P, 4 * HALF], BF16, name="x_grouped%d" % h, align_bytes=64)
+            for g in range(2):
+                back = psum.tile([P, 2, 2, P], F32, name="back", tag="tr")
+                for b in range(2):
+                    for u in range(2):
+                        nc.tensor.transpose(back[:, b, u, :], x_turned[h][:, 2 * g + b, u, :], ident32[:])
+                nc.scalar.copy(
+                    grouped[:].bitcast(F32)[:, 512 * g : 512 * (g + 1)].rearrange("p (b j u) -> p b j u", b=2, u=2),
+                    back[:].rearrange("p b u j -> p b j u"),
+                )
+            codes = keep.tile([P, HALF], U32, name="x_codes%d" % h, align_bytes=64)
+            plane = keep.tile([P, HALF], U8, name="x_plane%d" % h, align_bytes=64)
+            nc.vector.quantize_mx(out=codes[:].bitcast(FP8X4), scales=plane[:], in_=grouped[:])
+            x_grouped.append(grouped)
+            x_codes.append(codes)
+            x_planes.append(plane)
+        gather_sister(3, x_grouped[0][:].bitcast(F32))
+
+        def take_min(h, t):
+            y = psum.tile([P, HALF], F32, name="y", tag="mx")
+            nc.tensor.matmul_mx(
+                out=y[:], lhsT=wr_codes[:, P * t : P * (t + 1)].bitcast(FP8X4), lhsT_scale=wr_plane[:, P * t : P * (t + 1)],
+                rhs=x_codes[h][:].bitcast(FP8X4), rhs_scale=x_planes[h][:], start=True, stop=True,
+            )
+            lesser = ring.tile([P, HALF], F32, name="lesser", bufs=3)
+            nc.vector.scalar_tensor_tensor(
+                lesser[:], sisters[t][:, HALF * h : HALF * (h + 1)], sv_cols[:, t : t + 1], y[:], ALU.mult, ALU.min
+            )
+            return lesser
+
+        def add_and_store(h, t, lesser):
+            result = ring.tile([P, HALF], F32, name="result", bufs=3)
+            nc.vector.scalar_tensor_tensor(
+                result[:], sisters[t][:, HALF * h : HALF * (h + 1)], sv_cols[:, t : t + 1], lesser[:], ALU.mult, ALU.add
+            )
+            nc.sync.dma_start(out[P * t : P * (t + 1), HALF * h : HALF * (h + 1)], result[:])
+
+        pending = None
+        for t in range(TILES):
+            for h in range(2):
+                lesser = take_min(h, t)
+                if pending is not None:
+                    add_and_store(*pending)
+                pending = (h, t, lesser)
+        add_and_store(*pending)

@@ -46,12 +46,12 @@ def tile_list_swab_cavity_scores_kernel(
             return cols
 
         def load_table(a):
-            tab = keep.tile([P, T], I32, name="tab%d" % a)
+            tab = table_pool.tile([P, T], I32, name="tab%d" % a)
             nc.sync.dma_start(tab[:], tab_words[a].rearrange("p t i -> p (t i)").bitcast(I32))
             return tab
 
         def load_wa(t):
-            raw = keep.tile([P, 2048], F32, name="wa_raw%d" % t)
+            raw = keep.tile([P, PASSES * 512], F32, name="wa_raw%d" % t)
             for a in range(PASSES):
                 nc.sync.dma_start(
                     raw[:, 512 * a : 512 * (a + 1)].rearrange("p (j c) -> p j c", j=4),
@@ -64,91 +64,86 @@ def tile_list_swab_cavity_scores_kernel(
             nc.sync.dma_start(page[:], page0[P * t : P * (t + 1), :])
             return page
 
-        scale_win = keep.tile([P, T], U8, name="scale_win")
-        nc.vector.memset(scale_win[:].bitcast(I32), 0)
-        for q in range(4):
-            nc.gpsimd.dma_start(
-                scale_win[32 * q : 32 * q + 4 * PASSES, :].bitcast(I32),
-                tab_scales[:, 4 * q : 4 * q + 4, :].bitcast(I32),
+        with tc.tile_pool(name="table", bufs=1) as table_pool:
+            scale_win = table_pool.tile([P, T], U8, name="scale_win")
+            nc.vector.memset(scale_win[:].bitcast(I32), 0)
+            wb_planes = keep.tile([P, PASSES, H], U8, name="wb_planes", align_bytes=64)
+            nc.vector.memset(wb_planes[:].bitcast(I32), 0)
+            tab_planes = keep.tile([P, PASSES, S], U8, name="tab_planes", align_bytes=64)
+            nc.vector.memset(tab_planes[:].bitcast(I32), 0)
+
+            idx = load_list("idx", offs)
+            wa_raw = [load_wa(0)]
+            wb_codes = keep.tile([P, PASSES, 2 * H], U8, name="wb_codes", align_bytes=64)
+            nc.sync.dma_start(wb_codes[:].bitcast(I32), wb_words.rearrange("a p n -> p a n").bitcast(I32))
+            gain_cols = load_column_vector("gain_cols", gain)
+            nc.sync.dma_start(
+                scale_win[0:96:2, :].bitcast(I32), tab_scales.rearrange("a i t -> i a t").bitcast(I32)
             )
-        wb_planes = keep.tile([P, PASSES, H], U8, name="wb_planes", align_bytes=64)
-        nc.vector.memset(wb_planes[:].bitcast(I32), 0)
-        for q in range(4):
-            nc.gpsimd.dma_start(
-                wb_planes[32 * q : 32 * q + 4, :, :].bitcast(I32),
-                wb_scales[:, 4 * q : 4 * q + 4, :].rearrange("a r n -> r a n").bitcast(I32),
-            )
-        picked_scales = keep.tile([P, S], U8, name="picked_scales", align_bytes=64)
-        tab_planes = [picked_scales]
-        for a in range(1, PASSES):
-            plane = keep.tile([P, S], U8, name="tab_plane%d" % a, align_bytes=64)
-            nc.vector.memset(plane[:].bitcast(I32), 0)
-            tab_planes.append(plane)
+            tabs = [load_table(0)]
+            for q in range(4):
+                nc.sync.dma_start(
+                    wb_planes[32 * q : 32 * q + 4, :, :].bitcast(I32),
+                    wb_scales[:, 4 * q : 4 * q + 4, :].rearrange("a r n -> r a n").bitcast(I32),
+                )
+            tabs.append(load_table(1))
+            picked_scales = keep.tile([P, S], U8, name="picked_scales")
+            nc.vector.tensor_copy(picked_scales[:], scale_win[:].indirect(idx[:]))
+            for q in range(4):
+                nc.sync.dma_start(
+                    tab_planes[32 * q : 32 * q + 4, :, :].bitcast(I32),
+                    picked_scales[24 * q : 24 * q + 24 : 2, :].bitcast(I32),
+                )
+            tabs.append(load_table(2))
+            idx2 = load_list("idx2", offs2)
+            pages = [load_page(0)]
+            wgs_sb = keep.tile([P, S], F32, name="wgs_sb")
+            nc.sync.dma_start(wgs_sb[:, 0:HALF], wgs[:, 0:HALF])
+            wa_raw.append(load_wa(1))
+            nc.sync.dma_start(wgs_sb[:, HALF:S], wgs[:, HALF:S])
+            idx3 = load_list("idx3", offs3)
+            sx_cols = load_column_vector("sx_cols", sx)
+            idx4 = load_list("idx4", offs4)
+            sv_cols = load_column_vector("sv_cols", sv)
+            wa_raw.append(load_wa(2))
+            pages.append(load_page(1))
+            wa_raw.append(load_wa(3))
+            pages.append(load_page(2))
+            wr_raw = keep.tile([P, 4, H], F32, name="wr_raw")
+            nc.sync.dma_start(wr_raw[:], wr.rearrange("(p j) n -> p j n", j=4))
+            pages.append(load_page(3))
 
-        idx = load_list("idx", offs)
-        gain_cols = load_column_vector("gain_cols", gain)
-        tabs = [load_table(0)]
-        wa_raw = [load_wa(0)]
-        wb_codes = keep.tile([P, PASSES, 2 * H], U8, name="wb_codes", align_bytes=64)
-        nc.sync.dma_start(wb_codes[:].bitcast(I32), wb_words.rearrange("a p n -> p a n").bitcast(I32))
-        tabs.append(load_table(1))
-        tabs.append(load_table(2))
-        idx2 = load_list("idx2", offs2)
-        pages = [load_page(0)]
-        wgs_sb = keep.tile([P, S], F32, name="wgs_sb")
-        for h in range(2):
-            nc.sync.dma_start(wgs_sb[:, HALF * h : HALF * (h + 1)], wgs[:, HALF * h : HALF * (h + 1)])
-        idx3 = load_list("idx3", offs3)
-        sx_cols = load_column_vector("sx_cols", sx)
-        wa_raw.append(load_wa(1))
-        idx4 = load_list("idx4", offs4)
-        sv_cols = load_column_vector("sv_cols", sv)
-        wa_raw.append(load_wa(2))
-        pages.append(load_page(1))
-        wa_raw.append(load_wa(3))
-        pages.append(load_page(2))
-        wr_raw = keep.tile([P, 4, H], F32, name="wr_raw")
-        nc.sync.dma_start(wr_raw[:], wr.rearrange("(p j) n -> p j n", j=4))
-        pages.append(load_page(3))
+            ident32 = keep.tile([P, P], F32, name="ident32")
+            make_identity(nc, ident32[:])
+            ident16 = keep.tile([P, P], BF16, name="ident16")
+            make_identity(nc, ident16[:])
+            neg_gain = keep.tile([P, TILES], F32, name="neg_gain")
+            nc.vector.tensor_scalar(neg_gain[:], gain_cols[:], -1.0, None, ALU.mult)
 
-        ident32 = keep.tile([P, P], F32, name="ident32")
-        make_identity(nc, ident32[:])
-        ident16 = keep.tile([P, P], BF16, name="ident16")
-        make_identity(nc, ident16[:])
-        neg_gain = keep.tile([P, TILES], F32, name="neg_gain")
-        nc.vector.tensor_scalar(neg_gain[:], gain_cols[:], -1.0, None, ALU.mult)
+            picked = {}
+            for a in range(PASSES):
+                words = keep.tile([P, S], U32, name="picked%d" % a, align_bytes=64)
+                for h in range(2):
+                    half = words[:, HALF * h : HALF * (h + 1)]
+                    nc.vector.tensor_copy(half, tabs[a][:].bitcast(U32).indirect(idx[:, 32 * h : 32 * (h + 1)]))
+                    picked[a, h] = half
 
-        nc.vector.tensor_copy(picked_scales[:], scale_win[:].indirect(idx[:]))
-        for a in range(1, PASSES):
-            nc.gpsimd.dma_start(
-                tab_planes[a][0:100, :].bitcast(I32), picked_scales[4 * a : 4 * a + 100, :].bitcast(I32)
-            )
-        picked = {}
-        for a in range(PASSES):
-            words = keep.tile([P, S], U32, name="picked%d" % a, align_bytes=64)
-            for h in range(2):
-                half = words[:, HALF * h : HALF * (h + 1)]
-                nc.vector.tensor_copy(half, tabs[a][:].bitcast(U32).indirect(idx[:, 32 * h : 32 * (h + 1)]))
-                picked[a, h] = half
+        late = ctx.enter_context(tc.tile_pool(name="late", bufs=1))
 
-        LEFT = 256
-        boards = [keep.tile([P, LEFT + S + HALF], F32, name="board%d" % i, align_bytes=64) for i in range(2)]
+        SEAM = 1024
+        boards = [keep.tile([P, SEAM + 512], F32, name="board%d" % i, align_bytes=64) for i in range(TILES + 1)]
         first_staging = keep.tile([P, PASSES * 512], BF16, name="first_staging", align_bytes=64)
 
-        def staging(n, width):
-            if n == 0:
-                return first_staging[:]
-            board = boards[(n - 1) // 2]
-            words = width // 2
-            if n % 2 == 1:
-                return board[:, LEFT + HALF - words : LEFT + HALF].bitcast(BF16)
-            return board[:, LEFT + HALF : LEFT + HALF + words].bitcast(BF16)
+        def left_of_seam(t, width):
+            return boards[t][:, SEAM - width // 2 : SEAM].bitcast(BF16)
 
-        def quantize_wa(t):
-            grouped = staging(t, PASSES * 512)
+        def right_of_seam(t, width):
+            return boards[t][:, SEAM : SEAM + width // 2].bitcast(BF16)
+
+        def quantize_wa(t, grouped):
             nc.scalar.copy(
                 grouped.rearrange("p (a c i j) -> p a c j i", a=PASSES, i=4, j=4),
-                wa_raw[t][:, 0 : PASSES * 512].rearrange("p (a j c i) -> p a c j i", a=PASSES, i=4, j=4),
+                wa_raw[t][:].rearrange("p (a j c i) -> p a c j i", a=PASSES, i=4, j=4),
             )
             codes = keep.tile([P, PASSES * P], U32, name="wa_codes%d" % t, align_bytes=64)
             planes = keep.tile([P, PASSES * P], U8, name="wa_planes%d" % t, align_bytes=64)
@@ -160,8 +155,7 @@ def tile_list_swab_cavity_scores_kernel(
                 )
             return codes, planes
 
-        def quantize_wr():
-            grouped = staging(TILES, 4 * H)
+        def quantize_wr(grouped):
             nc.scalar.copy(
                 grouped.rearrange("p (c i j) -> p c j i", i=4, j=4),
                 wr_raw[:].rearrange("p j (c i) -> p c j i", i=4),
@@ -171,44 +165,42 @@ def tile_list_swab_cavity_scores_kernel(
             nc.vector.quantize_mx(out=codes[:].bitcast(FP8X4), scales=plane[:], in_=grouped)
             return codes, plane
 
-        def first_stage(t, wa_codes, wa_planes):
-            entries = boards[t % 2][:, LEFT : LEFT + S]
-            for h in range(2):
-                warm = psum.tile([P, HALF], F32, name="warm", tag="mx")
-                wear = psum.tile([P, HALF], F32, name="wear", tag="mx")
+        def first_stage(t, h, magnitude, entries):
+            wa_codes, wa_planes = quantized[t]
+            warm = psum.tile([P, HALF], F32, name="warm", tag="mx")
+            wear = psum.tile([P, HALF], F32, name="wear", tag="mx")
+            for bank in (warm, wear):
                 for a in range(PASSES):
+                    if bank is warm:
+                        rhs = wa_codes[:, P * a : P * (a + 1)].bitcast(FP8X4)
+                        rhs_scale = wa_planes[:, P * a : P * (a + 1)]
+                    else:
+                        rhs = wb_codes[:, a, 2 * P * t : 2 * P * (t + 1)].bitcast(FP4X4)
+                        rhs_scale = wb_planes[:, a, P * t : P * (t + 1)]
                     for b in range(SUB):
-                        first = a == 0 and b == 0
-                        last = a == PASSES - 1 and b == SUB - 1
-                        lhs = picked[a, h][:, P * b : P * (b + 1)].bitcast(FP8X4)
-                        lhs_scale = tab_planes[a][:, HALF * h + P * b : HALF * h + P * (b + 1)]
                         nc.tensor.matmul_mx(
-                            out=warm[:, P * b : P * (b + 1)], lhsT=lhs, lhsT_scale=lhs_scale,
-                            rhs=wa_codes[:, P * a : P * (a + 1)].bitcast(FP8X4),
-                            rhs_scale=wa_planes[:, P * a : P * (a + 1)],
-                            start=first, stop=last,
+                            out=bank[:, P * b : P * (b + 1)],
+                            lhsT=picked[a, h][:, P * b : P * (b + 1)].bitcast(FP8X4),
+                            lhsT_scale=tab_planes[:, a, HALF * h + P * b : HALF * h + P * (b + 1)],
+                            rhs=rhs, rhs_scale=rhs_scale,
+                            start=(a == 0 and b == 0), stop=(a == PASSES - 1 and b == SUB - 1),
                         )
-                        nc.tensor.matmul_mx(
-                            out=wear[:, P * b : P * (b + 1)], lhsT=lhs, lhsT_scale=lhs_scale,
-                            rhs=wb_codes[:, a, 2 * P * t : 2 * P * (t + 1)].bitcast(FP4X4),
-                            rhs_scale=wb_planes[:, a, P * t : P * (t + 1)],
-                            start=first, stop=last,
-                        )
-                neg_tanh = ring.tile([P, HALF], F32, name="neg_tanh")
-                nc.scalar.activation(neg_tanh[:], warm[:], ACT.Tanh, scale=-1.0)
-                magnitude = ring.tile([P, HALF], F32, name="magnitude", bufs=3)
-                nc.scalar.activation(magnitude[:], wear[:], ACT.Abs)
-                turned = psum.tile([P, HALF], F32, name="turned", tag="tr")
+            neg_tanh = ring.tile([P, HALF], F32, name="neg_tanh")
+            nc.scalar.activation(neg_tanh[:], warm[:], ACT.Tanh, scale=-1.0)
+            nc.scalar.activation(magnitude, wear[:], ACT.Abs)
+            turned = psum.tile([P, HALF], F32, name="turned", tag="tr")
+            for i, term in enumerate((neg_tanh[:], magnitude)):
                 for b in range(SUB):
                     cols = slice(P * b, P * (b + 1))
-                    nc.tensor.matmul(turned[:, cols], neg_tanh[:, cols], ident32[:], start=True, stop=False, is_transpose=True)
-                    nc.tensor.matmul(turned[:, cols], magnitude[:, cols], ident32[:], start=False, stop=True, is_transpose=True)
-                nc.scalar.activation(
-                    entries[:, HALF * h : HALF * (h + 1)], turned[:], ACT.Copy, scale=neg_gain[:, t : t + 1]
-                )
-            return entries, magnitude
+                    nc.tensor.matmul(
+                        turned[:, cols], term[:, cols], ident32[:], is_transpose=True,
+                        start=(i == 0 and b == 0), stop=(i == 1 and b == SUB - 1),
+                    )
+            nc.scalar.activation(
+                entries, turned[:], ACT.Copy, scale=neg_gain[:, t : t + 1]
+            )
 
-        x_turned = [keep.tile([P, SUB, 2, P], F32, name="x_turned%d" % h) for h in range(2)]
+        x_turned = [late.tile([P, SUB, 2, P], F32, name="x_turned%d" % h) for h in range(2)]
         sisters = {}
 
         def gather_sister(t, dst):
@@ -218,49 +210,73 @@ def tile_list_swab_cavity_scores_kernel(
         def put(t, h, entries):
             cols = slice(HALF * h, HALF * (h + 1))
             nc.vector.tensor_tensor(
-                pages[t][:].indirect(idx2[:, 32 * h : 32 * (h + 1)]), entries[:, cols], wgs_sb[:, cols], ALU.mult
+                pages[t][:].indirect(idx2[:, 32 * h : 32 * (h + 1)]), entries, wgs_sb[:, cols], ALU.mult
             )
 
-        def turn_x(t, spare, due):
+        def turn_x(t, x_rows, due, pieces):
+            n = NP // pieces
+            for i in range(pieces):
+                cols = slice(i * n, (i + 1) * n)
+                nc.scalar.activation(x_rows[:, cols], due[:, cols], ACT.Copy, scale=sx_cols[:, t : t + 1])
             for h in range(2):
-                x_rows = spare[:, 256 * h : 256 * (h + 1)].bitcast(BF16)
-                nc.scalar.activation(x_rows, due[:, HALF * h : HALF * (h + 1)], ACT.Copy, scale=sx_cols[:, t : t + 1])
                 x_cols = psum.tile([P, SUB, P], BF16, name="x_cols", tag="tr")
                 for b in range(SUB):
-                    nc.tensor.transpose(x_cols[:, b, :], x_rows[:, P * b : P * (b + 1)], ident16[:])
+                    c0 = HALF * h + P * b
+                    nc.tensor.transpose(x_cols[:, b, :], x_rows[:, c0 : c0 + P], ident16[:])
                 nc.scalar.copy(
                     x_turned[h][:, :, :, 32 * t : 32 * (t + 1)],
                     x_cols[:].bitcast(F32).rearrange("p b (q u) -> p b u q", u=2),
                 )
 
-        quantized = [quantize_wa(0)]
-        entries, spare = first_stage(0, *quantized[0])
+        def on_seam(i):
+            return boards[i][:, SEAM + 64 - HALF : SEAM + 64]
+
+        def both_halves(t):
+            entries = ring.tile([P, S], F32, name="entries")
+            magnitude = ring.tile([P, HALF], F32, name="magnitude")
+            first_stage(t, 0, magnitude[:], entries[:, 0:HALF])
+            first_stage(t, 1, on_seam(t), entries[:, HALF:S])
+            return entries
+
+        WA_WIDTH = PASSES * 512
+        quantized = [quantize_wa(0, first_staging[:])]
+        opening = ring.tile([P, S], F32, name="entries")
+        first_stage(0, 0, on_seam(TILES), opening[:, 0:HALF])
+        quantized.append(quantize_wa(1, left_of_seam(TILES, WA_WIDTH)))
+        halves = [opening[:, 0:HALF], wa_raw[1][:, 2 * HALF : 3 * HALF]]
+        first_stage(0, 1, on_seam(0), halves[1])
+        last_rows = late.tile([P, NP], BF16, name="last_rows")
+        first_sister = late.tile([P, NP], F32, name="first_sister")
         for t in range(TILES):
             for h in range(2):
-                put(t, h, entries)
-                n = 2 * t + h + 1
-                if n < TILES:
-                    quantized.append(quantize_wa(n))
-                elif n == TILES:
-                    wr_codes, wr_plane = quantize_wr()
-            due = wa_raw[(t + 1) % TILES][:, 0:NP]
-            get_pieces = 2 if t == TILES - 1 else 1
-            for i in range(get_pieces):
-                n = NP // get_pieces
+                put(t, h, halves[h])
+            if t == 0:
+                quantized.append(quantize_wa(2, left_of_seam(0, WA_WIDTH)))
+            elif t == 1:
+                quantized.append(quantize_wa(3, left_of_seam(1, WA_WIDTH)))
+            elif t == 3:
+                wr_codes, wr_plane = quantize_wr(left_of_seam(3, 4 * H))
+            due = wa_raw[(0, 3, 2, 1)[t]][:, 0:NP]
+            pieces = 2 if t == TILES - 1 else 1
+            for i in range(pieces):
+                n = NP // pieces
                 nc.vector.tensor_copy(
                     due[:, i * n : (i + 1) * n], pages[t][:].indirect(idx3[:, i * n // 16 : (i + 1) * n // 16])
                 )
             if t == 0:
-                gather_sister(0, wa_raw[1][:, NP : 2 * NP])
+                gather_sister(0, first_sister[:])
             if t + 1 < TILES:
-                entries, spare = first_stage(t + 1, *quantized[t + 1])
-            turn_x(t, spare, due)
+                entries = both_halves(t + 1)
+                halves = [entries[:, 0:HALF], entries[:, HALF:S]]
+                turn_x(t, right_of_seam(t + 1, NP), due, pieces)
+            else:
+                turn_x(t, last_rows[:], due, pieces)
         gather_sister(1, wgs_sb[:])
-        gather_sister(2, entries)
+        gather_sister(2, entries[:])
 
         x_grouped, x_codes, x_planes = [], [], []
         for h in range(2):
-            grouped = keep.tile([P, 4 * HALF], BF16, name="x_grouped%d" % h, align_bytes=64)
+            grouped = late.tile([P, 4 * HALF], BF16, name="x_grouped%d" % h, align_bytes=64)
             for g in range(2):
                 back = psum.tile([P, 2, 2, P], F32, name="back", tag="tr")
                 for b in range(2):
@@ -270,8 +286,8 @@ def tile_list_swab_cavity_scores_kernel(
                     grouped[:].bitcast(F32)[:, 512 * g : 512 * (g + 1)].rearrange("p (b j u) -> p b j u", b=2, u=2),
                     back[:].rearrange("p b u j -> p b j u"),
                 )
-            codes = keep.tile([P, HALF], U32, name="x_codes%d" % h, align_bytes=64)
-            plane = keep.tile([P, HALF], U8, name="x_plane%d" % h, align_bytes=64)
+            codes = late.tile([P, HALF], U32, name="x_codes%d" % h, align_bytes=64)
+            plane = late.tile([P, HALF], U8, name="x_plane%d" % h, align_bytes=64)
             nc.vector.quantize_mx(out=codes[:].bitcast(FP8X4), scales=plane[:], in_=grouped[:])
             x_grouped.append(grouped)
             x_codes.append(codes)
@@ -284,22 +300,22 @@ def tile_list_swab_cavity_scores_kernel(
                 out=y[:], lhsT=wr_codes[:, P * t : P * (t + 1)].bitcast(FP8X4), lhsT_scale=wr_plane[:, P * t : P * (t + 1)],
                 rhs=x_codes[h][:].bitcast(FP8X4), rhs_scale=x_planes[h][:], start=True, stop=True,
             )
-            lesser = ring.tile([P, HALF], F32, name="lesser", bufs=3)
+            lesser = late.tile([P, HALF], F32, name="lesser", bufs=3)
             nc.vector.scalar_tensor_tensor(
                 lesser[:], sisters[t][:, HALF * h : HALF * (h + 1)], sv_cols[:, t : t + 1], y[:], ALU.mult, ALU.min
             )
             return lesser
 
         def add_and_store(h, t, lesser):
-            result = ring.tile([P, HALF], F32, name="result", bufs=3)
+            result = late.tile([P, HALF], F32, name="result", bufs=3)
             nc.vector.scalar_tensor_tensor(
                 result[:], sisters[t][:, HALF * h : HALF * (h + 1)], sv_cols[:, t : t + 1], lesser[:], ALU.mult, ALU.add
             )
             nc.sync.dma_start(out[P * t : P * (t + 1), HALF * h : HALF * (h + 1)], result[:])
 
         pending = None
-        for t in range(TILES):
-            for h in range(2):
+        for h in range(2):
+            for t in range(TILES):
                 lesser = take_min(h, t)
                 if pending is not None:
                     add_and_store(*pending)

@@ -39,12 +39,6 @@ def tile_list_swab_cavity_scores_kernel(
             nc.sync.dma_start(lst[:], src)
             return lst
 
-        def load_column_vector(name, src):
-            cols = keep.tile([P, TILES], F32, name=name)
-            with nc.allow_non_contiguous_dma(reason="one value a partition"):
-                nc.sync.dma_start(cols[:], src.rearrange("(t p) -> p t", p=P))
-            return cols
-
         def load_table(a):
             tab = table_pool.tile([P, T], I32, name="tab%d" % a)
             nc.sync.dma_start(tab[:], tab_words[a].rearrange("p t i -> p (t i)").bitcast(I32))
@@ -58,6 +52,17 @@ def tile_list_swab_cavity_scores_kernel(
                     wa[512 * a : 512 * (a + 1), P * t : P * (t + 1)].rearrange("(p j) c -> p j c", j=4),
                 )
             return raw
+
+        def load_wb(name, t0, t1):
+            codes = keep.tile([P, PASSES, 2 * P * (t1 - t0)], U8, name=name, align_bytes=64)
+            nc.sync.dma_start(
+                codes[:].bitcast(I32),
+                wb_words[:, :, 2 * P * t0 : 2 * P * t1].rearrange("a p n -> p a n").bitcast(I32),
+            )
+            return codes
+
+        def load_vector_rows(rows, i, vec):
+            nc.sync.dma_start(rows[TILES * i : TILES * (i + 1), :], vec.rearrange("(t p) -> t p", p=P))
 
         def load_page(t):
             page = keep.tile([P, T2], F32, name="page%d" % t)
@@ -74,9 +79,9 @@ def tile_list_swab_cavity_scores_kernel(
 
             idx = load_list("idx", offs)
             wa_raw = [load_wa(0)]
-            wb_codes = keep.tile([P, PASSES, 2 * H], U8, name="wb_codes", align_bytes=64)
-            nc.sync.dma_start(wb_codes[:].bitcast(I32), wb_words.rearrange("a p n -> p a n").bitcast(I32))
-            gain_cols = load_column_vector("gain_cols", gain)
+            wb_first = load_wb("wb_first", 0, 1)
+            vector_rows = keep.tile([P, P], F32, name="vector_rows")
+            nc.gpsimd.memset(vector_rows[:], 0.0)
             nc.sync.dma_start(
                 scale_win[0:96:2, :].bitcast(I32), tab_scales.rearrange("a i t -> i a t").bitcast(I32)
             )
@@ -86,7 +91,10 @@ def tile_list_swab_cavity_scores_kernel(
                     wb_planes[32 * q : 32 * q + 4, :, :].bitcast(I32),
                     wb_scales[:, 4 * q : 4 * q + 4, :].rearrange("a r n -> r a n").bitcast(I32),
                 )
+            load_vector_rows(vector_rows, 0, gain)
+            load_vector_rows(vector_rows, 1, sx)
             tabs.append(load_table(1))
+            load_vector_rows(vector_rows, 2, sv)
             picked_scales = keep.tile([P, S], U8, name="picked_scales")
             nc.vector.tensor_copy(picked_scales[:], scale_win[:].indirect(idx[:]))
             for q in range(4):
@@ -101,32 +109,36 @@ def tile_list_swab_cavity_scores_kernel(
             nc.sync.dma_start(wgs_sb[:, 0:HALF], wgs[:, 0:HALF])
             wa_raw.append(load_wa(1))
             nc.sync.dma_start(wgs_sb[:, HALF:S], wgs[:, HALF:S])
+            wb_rest = load_wb("wb_rest", 1, TILES)
             idx3 = load_list("idx3", offs3)
-            sx_cols = load_column_vector("sx_cols", sx)
             idx4 = load_list("idx4", offs4)
-            sv_cols = load_column_vector("sv_cols", sv)
             wa_raw.append(load_wa(2))
             pages.append(load_page(1))
             wa_raw.append(load_wa(3))
             pages.append(load_page(2))
-            wr_raw = keep.tile([P, 4, H], F32, name="wr_raw")
-            nc.sync.dma_start(wr_raw[:], wr.rearrange("(p j) n -> p j n", j=4))
+            wr_raw = keep.tile([P, 4 * H], F32, name="wr_raw")
+            nc.sync.dma_start(wr_raw[:], wr.rearrange("(p j) n -> p (j n)", j=4))
             pages.append(load_page(3))
 
             ident32 = keep.tile([P, P], F32, name="ident32")
             make_identity(nc, ident32[:])
             ident16 = keep.tile([P, P], BF16, name="ident16")
             make_identity(nc, ident16[:])
+            vector_cols = psum.tile([P, P], F32, name="vector_cols", tag="tr")
+            nc.tensor.transpose(vector_cols[:], vector_rows[:], ident32[:])
             neg_gain = keep.tile([P, TILES], F32, name="neg_gain")
-            nc.vector.tensor_scalar(neg_gain[:], gain_cols[:], -1.0, None, ALU.mult)
+            nc.vector.tensor_scalar(neg_gain[:], vector_cols[:, 0:TILES], -1.0, None, ALU.mult)
+            factors = keep.tile([P, 2 * TILES], F32, name="factors")
+            nc.vector.tensor_copy(factors[:], vector_cols[:, TILES : 3 * TILES])
+            sx_cols, sv_cols = factors[:, 0:TILES], factors[:, TILES : 2 * TILES]
 
-            picked = {}
+            picked = []
             for a in range(PASSES):
                 words = keep.tile([P, S], U32, name="picked%d" % a, align_bytes=64)
                 for h in range(2):
                     half = words[:, HALF * h : HALF * (h + 1)]
                     nc.vector.tensor_copy(half, tabs[a][:].bitcast(U32).indirect(idx[:, 32 * h : 32 * (h + 1)]))
-                    picked[a, h] = half
+                picked.append(words)
 
         late = ctx.enter_context(tc.tile_pool(name="late", bufs=1))
 
@@ -158,59 +170,85 @@ def tile_list_swab_cavity_scores_kernel(
         def quantize_wr(grouped):
             nc.scalar.copy(
                 grouped.rearrange("p (c i j) -> p c j i", i=4, j=4),
-                wr_raw[:].rearrange("p j (c i) -> p c j i", i=4),
+                wr_raw[:].rearrange("p (j c i) -> p c j i", j=4, i=4),
             )
             codes = keep.tile([P, H], U32, name="wr_codes", align_bytes=64)
             plane = keep.tile([P, H], U8, name="wr_plane", align_bytes=64)
             nc.vector.quantize_mx(out=codes[:].bitcast(FP8X4), scales=plane[:], in_=grouped)
             return codes, plane
 
-        def first_stage(t, h, magnitude, entries):
-            wa_codes, wa_planes = quantized[t]
-            warm = psum.tile([P, HALF], F32, name="warm", tag="mx")
-            wear = psum.tile([P, HALF], F32, name="wear", tag="mx")
-            for bank in (warm, wear):
+        def open_sums(n):
+            if 2 * n <= HALF:
+                bank = psum.tile([P, 2 * n], F32, name="both", tag="mx")
+                return bank[:, 0:n], bank[:, n : 2 * n]
+            warm = psum.tile([P, n], F32, name="warm", tag="mx")
+            wear = psum.tile([P, n], F32, name="wear", tag="mx")
+            return warm[:], wear[:]
+
+        def multiply(t, j0, n, sums, which, a):
+            shared = 2 * n <= HALF
+            if which == 0:
+                wa_codes, wa_planes = quantized[t]
+                rhs = wa_codes[:, P * a : P * (a + 1)].bitcast(FP8X4)
+                rhs_scale = wa_planes[:, P * a : P * (a + 1)]
+            else:
+                wb_codes = wb_first[:, a, :] if t == 0 else wb_rest[:, a, 2 * P * (t - 1) : 2 * P * t]
+                rhs = wb_codes.bitcast(FP4X4)
+                rhs_scale = wb_planes[:, a, P * t : P * (t + 1)]
+            blocks = n // P
+            for b in range(blocks):
+                cols = slice(j0 + P * b, j0 + P * (b + 1))
+                nc.tensor.matmul_mx(
+                    out=sums[which][:, P * b : P * (b + 1)],
+                    lhsT=picked[a][:, cols].bitcast(FP8X4), lhsT_scale=tab_planes[:, a, cols],
+                    rhs=rhs, rhs_scale=rhs_scale,
+                    start=(a == 0 and b == 0 and not (shared and which == 1)),
+                    stop=(a == PASSES - 1 and b == blocks - 1 and not (shared and which == 0)),
+                )
+
+        def first_stage(t, j0, n, magnitude, entries):
+            sums = open_sums(n)
+            for which in range(2):
                 for a in range(PASSES):
-                    if bank is warm:
-                        rhs = wa_codes[:, P * a : P * (a + 1)].bitcast(FP8X4)
-                        rhs_scale = wa_planes[:, P * a : P * (a + 1)]
-                    else:
-                        rhs = wb_codes[:, a, 2 * P * t : 2 * P * (t + 1)].bitcast(FP4X4)
-                        rhs_scale = wb_planes[:, a, P * t : P * (t + 1)]
-                    for b in range(SUB):
-                        nc.tensor.matmul_mx(
-                            out=bank[:, P * b : P * (b + 1)],
-                            lhsT=picked[a, h][:, P * b : P * (b + 1)].bitcast(FP8X4),
-                            lhsT_scale=tab_planes[:, a, HALF * h + P * b : HALF * h + P * (b + 1)],
-                            rhs=rhs, rhs_scale=rhs_scale,
-                            start=(a == 0 and b == 0), stop=(a == PASSES - 1 and b == SUB - 1),
-                        )
-            neg_tanh = ring.tile([P, HALF], F32, name="neg_tanh")
-            nc.scalar.activation(neg_tanh[:], warm[:], ACT.Tanh, scale=-1.0)
-            nc.scalar.activation(magnitude, wear[:], ACT.Abs)
-            turned = psum.tile([P, HALF], F32, name="turned", tag="tr")
+                    multiply(t, j0, n, sums, which, a)
+            make_entries(t, n, sums, magnitude, entries)
+
+        def make_entries(t, n, sums, magnitude, entries):
+            warm, wear = sums
+            blocks = n // P
+            neg_tanh = ring.tile([P, n], F32, name="neg_tanh")
+            nc.scalar.activation(neg_tanh[:], warm, ACT.Tanh, scale=-1.0)
+            nc.scalar.activation(magnitude, wear, ACT.Abs)
+            turned = psum.tile([P, n], F32, name="turned", tag="tr")
             for i, term in enumerate((neg_tanh[:], magnitude)):
-                for b in range(SUB):
+                for b in range(blocks):
                     cols = slice(P * b, P * (b + 1))
                     nc.tensor.matmul(
                         turned[:, cols], term[:, cols], ident32[:], is_transpose=True,
-                        start=(i == 0 and b == 0), stop=(i == 1 and b == SUB - 1),
+                        start=(i == 0 and b == 0), stop=(i == 1 and b == blocks - 1),
                     )
-            nc.scalar.activation(
-                entries, turned[:], ACT.Copy, scale=neg_gain[:, t : t + 1]
-            )
+            nc.scalar.activation(entries, turned[:], ACT.Copy, scale=neg_gain[:, t : t + 1])
 
-        x_turned = [late.tile([P, SUB, 2, P], F32, name="x_turned%d" % h) for h in range(2)]
+        wide = late.tile([P, 2 * NP], F32, name="wide")
+        narrow = late.tile([P, NP], F32, name="narrow")
+        x_turned = [
+            flat.rearrange("p (b u q) -> p b u q", b=SUB, u=2) for flat in (narrow[:], wide[:, 64 : 64 + NP])
+        ]
         sisters = {}
 
         def gather_sister(t, dst):
             nc.vector.tensor_copy(dst, pages[t][:].indirect(idx4[:]))
             sisters[t] = dst
 
-        def put(t, h, entries):
-            cols = slice(HALF * h, HALF * (h + 1))
+        scaled = {}
+
+        def scale_sister(t, dst):
+            nc.scalar.activation(dst, sisters[t], ACT.Copy, scale=sv_cols[:, t : t + 1])
+            scaled[t] = dst
+
+        def put(t, j0, n, entries):
             nc.vector.tensor_tensor(
-                pages[t][:].indirect(idx2[:, 32 * h : 32 * (h + 1)]), entries, wgs_sb[:, cols], ALU.mult
+                pages[t][:].indirect(idx2[:, j0 // 16 : (j0 + n) // 16]), entries, wgs_sb[:, j0 : j0 + n], ALU.mult
             )
 
         def turn_x(t, x_rows, due, pieces):
@@ -228,35 +266,43 @@ def tile_list_swab_cavity_scores_kernel(
                     x_cols[:].bitcast(F32).rearrange("p b (q u) -> p b u q", u=2),
                 )
 
-        def on_seam(i):
-            return boards[i][:, SEAM + 64 - HALF : SEAM + 64]
+        def on_seam(i, n=HALF):
+            return boards[i][:, SEAM + 64 - n : SEAM + 64]
 
         def both_halves(t):
             entries = ring.tile([P, S], F32, name="entries")
             magnitude = ring.tile([P, HALF], F32, name="magnitude")
-            first_stage(t, 0, magnitude[:], entries[:, 0:HALF])
-            first_stage(t, 1, on_seam(t), entries[:, HALF:S])
+            first_stage(t, 0, HALF, magnitude[:], entries[:, 0:HALF])
+            first_stage(t, HALF, HALF, on_seam(t), entries[:, HALF:S])
             return entries
 
         WA_WIDTH = PASSES * 512
         quantized = [quantize_wa(0, first_staging[:])]
         opening = ring.tile([P, S], F32, name="entries")
-        first_stage(0, 0, on_seam(TILES), opening[:, 0:HALF])
+        QUARTER = HALF // 2
+        spans = [(0, QUARTER), (QUARTER, QUARTER), (HALF, HALF)]
+        opening_sums = [open_sums(n) for j0, n in spans]
+        for a in range(PASSES):
+            for (j0, n), sums in zip(spans, opening_sums):
+                for which in range(2):
+                    multiply(0, j0, n, sums, which, a)
+        first_magnitude = ring.tile([P, QUARTER], F32, name="magnitude")
+        make_entries(0, QUARTER, opening_sums[0], first_magnitude[:], opening[:, 0:QUARTER])
+        make_entries(0, QUARTER, opening_sums[1], on_seam(TILES, QUARTER), opening[:, QUARTER:HALF])
         quantized.append(quantize_wa(1, left_of_seam(TILES, WA_WIDTH)))
-        halves = [opening[:, 0:HALF], wa_raw[1][:, 2 * HALF : 3 * HALF]]
-        first_stage(0, 1, on_seam(0), halves[1])
+        second_half = wa_raw[1][:, 2 * HALF : 3 * HALF]
+        make_entries(0, HALF, opening_sums[2], on_seam(0), second_half)
+        parts = [(0, QUARTER, opening[:, 0:QUARTER]), (QUARTER, QUARTER, opening[:, QUARTER:HALF]), (HALF, HALF, second_half)]
         last_rows = late.tile([P, NP], BF16, name="last_rows")
         first_sister = late.tile([P, NP], F32, name="first_sister")
         for t in range(TILES):
-            for h in range(2):
-                put(t, h, halves[h])
+            for part in parts:
+                put(t, *part)
             if t == 0:
                 quantized.append(quantize_wa(2, left_of_seam(0, WA_WIDTH)))
             elif t == 1:
                 quantized.append(quantize_wa(3, left_of_seam(1, WA_WIDTH)))
-            elif t == 3:
-                wr_codes, wr_plane = quantize_wr(left_of_seam(3, 4 * H))
-            due = wa_raw[(0, 3, 2, 1)[t]][:, 0:NP]
+            due = (wa_raw[0], wa_raw[3], wr_raw, wa_raw[1])[t][:, 0:NP]
             pieces = 2 if t == TILES - 1 else 1
             for i in range(pieces):
                 n = NP // pieces
@@ -267,10 +313,17 @@ def tile_list_swab_cavity_scores_kernel(
                 gather_sister(0, first_sister[:])
             if t + 1 < TILES:
                 entries = both_halves(t + 1)
-                halves = [entries[:, 0:HALF], entries[:, HALF:S]]
+                if t == 0:
+                    parts = [(0, HALF, entries[:, 0:HALF]), (HALF, HALF, entries[:, HALF:S])]
+                else:
+                    parts = [(0, S, entries[:])]
+                if t == 1:
+                    wr_codes, wr_plane = quantize_wr(left_of_seam(2, 4 * H))
                 turn_x(t, right_of_seam(t + 1, NP), due, pieces)
             else:
                 turn_x(t, last_rows[:], due, pieces)
+            if t == 0:
+                scale_sister(0, due)
         gather_sister(1, wgs_sb[:])
         gather_sister(2, entries[:])
 
@@ -292,32 +345,37 @@ def tile_list_swab_cavity_scores_kernel(
             x_grouped.append(grouped)
             x_codes.append(codes)
             x_planes.append(plane)
-        gather_sister(3, x_grouped[0][:].bitcast(F32))
+        scale_sister(1, wide[:, 0:NP])
+        scale_sister(2, wide[:, NP : 2 * NP])
 
-        def take_min(h, t):
+        def take_min(t, h):
             y = psum.tile([P, HALF], F32, name="y", tag="mx")
             nc.tensor.matmul_mx(
                 out=y[:], lhsT=wr_codes[:, P * t : P * (t + 1)].bitcast(FP8X4), lhsT_scale=wr_plane[:, P * t : P * (t + 1)],
                 rhs=x_codes[h][:].bitcast(FP8X4), rhs_scale=x_planes[h][:], start=True, stop=True,
             )
-            lesser = late.tile([P, HALF], F32, name="lesser", bufs=3)
+            lesser = late.tile([P, HALF], F32, name="lesser%d_%d" % (t, h))
             nc.vector.scalar_tensor_tensor(
                 lesser[:], sisters[t][:, HALF * h : HALF * (h + 1)], sv_cols[:, t : t + 1], y[:], ALU.mult, ALU.min
             )
             return lesser
 
-        def add_and_store(h, t, lesser):
-            result = late.tile([P, HALF], F32, name="result", bufs=3)
-            nc.vector.scalar_tensor_tensor(
-                result[:], sisters[t][:, HALF * h : HALF * (h + 1)], sv_cols[:, t : t + 1], lesser[:], ALU.mult, ALU.add
-            )
-            nc.sync.dma_start(out[P * t : P * (t + 1), HALF * h : HALF * (h + 1)], result[:])
+        def add_and_store(t, h, lesser, engine):
+            cols = slice(HALF * h, HALF * (h + 1))
+            result = late.tile([P, HALF], F32, name="result", bufs=4)
+            if t in scaled:
+                engine.tensor_tensor(result[:], lesser[:], scaled[t][:, cols], ALU.add)
+            else:
+                engine.scalar_tensor_tensor(
+                    result[:], sisters[t][:, cols], sv_cols[:, t : t + 1], lesser[:], ALU.mult, ALU.add
+                )
+            nc.sync.dma_start(out[P * t : P * (t + 1), cols], result[:])
 
-        pending = None
         for h in range(2):
-            for t in range(TILES):
-                lesser = take_min(h, t)
-                if pending is not None:
-                    add_and_store(*pending)
-                pending = (h, t, lesser)
-        add_and_store(*pending)
+            for t in range(TILES - 1):
+                add_and_store(t, h, take_min(t, h), nc.gpsimd)
+        last = TILES - 1
+        gather_sister(last, sisters[last - 1])
+        lessers = [take_min(last, h) for h in range(2)]
+        for h in range(2):
+            add_and_store(last, h, lessers[h], nc.vector)

@@ -18,10 +18,20 @@ ALU = mybir.AluOpType
 ACT = mybir.ActivationFunctionType
 
 P = 128
-PASSES = K // 512
+PACK = 4
+K_PASS = P * PACK
+PASSES = K // K_PASS
 TILES = H // P
+LAST = TILES - 1
+QUADRANTS = 4
+LIST_ROWS = 16
 HALF = 512
-SUB = HALF // P
+QUARTER = HALF // 2
+BLOCKS = HALF // P
+WA_WIDTH = PASSES * K_PASS
+WARM, WEAR = 0, 1
+SEAM = 1024
+OVERLAP = P // 2
 
 
 def tile_list_swab_cavity_scores_kernel(
@@ -34,10 +44,13 @@ def tile_list_swab_cavity_scores_kernel(
         ring = ctx.enter_context(tc.tile_pool(name="ring", bufs=2))
         psum = ctx.enter_context(tc.psum_pool(name="psum", bufs=4))
 
-        def load_list(name, src):
-            lst = keep.tile([P, S // 16], U16, name=name)
-            nc.sync.dma_start(lst[:], src)
-            return lst
+        def entries_of(offsets, j0, count):
+            return offsets[:, j0 // LIST_ROWS : (j0 + count) // LIST_ROWS]
+
+        def load_list(name, source):
+            offsets = keep.tile([P, S // LIST_ROWS], U16, name=name)
+            nc.sync.dma_start(offsets[:], source)
+            return offsets
 
         def load_table(a):
             tab = table_pool.tile([P, T], I32, name="tab%d" % a)
@@ -45,11 +58,12 @@ def tile_list_swab_cavity_scores_kernel(
             return tab
 
         def load_wa(t):
-            raw = keep.tile([P, PASSES * 512], F32, name="wa_raw%d" % t)
+            raw = keep.tile([P, WA_WIDTH], F32, name="wa_raw%d" % t, align_bytes=64)
             for a in range(PASSES):
+                rows = slice(K_PASS * a, K_PASS * (a + 1))
                 nc.sync.dma_start(
-                    raw[:, 512 * a : 512 * (a + 1)].rearrange("p (j c) -> p j c", j=4),
-                    wa[512 * a : 512 * (a + 1), P * t : P * (t + 1)].rearrange("(p j) c -> p j c", j=4),
+                    raw[:, rows].rearrange("p (i c) -> p i c", i=PACK),
+                    wa[rows, P * t : P * (t + 1)].rearrange("(p i) c -> p i c", i=PACK),
                 )
             return raw
 
@@ -57,12 +71,13 @@ def tile_list_swab_cavity_scores_kernel(
             codes = keep.tile([P, PASSES, 2 * P * (t1 - t0)], U8, name=name, align_bytes=64)
             nc.sync.dma_start(
                 codes[:].bitcast(I32),
-                wb_words[:, :, 2 * P * t0 : 2 * P * t1].rearrange("a p n -> p a n").bitcast(I32),
+                wb_words[:, :, 2 * P * t0 : 2 * P * t1].rearrange("a p c -> p a c").bitcast(I32),
             )
             return codes
 
-        def load_vector_rows(rows, i, vec):
-            nc.sync.dma_start(rows[TILES * i : TILES * (i + 1), :], vec.rearrange("(t p) -> t p", p=P))
+        def load_vector_rows(place, vector):
+            rows = vector_rows[TILES * place : TILES * (place + 1), :]
+            nc.sync.dma_start(rows, vector.rearrange("(t p) -> t p", p=P))
 
         def load_page(t):
             page = keep.tile([P, T2], F32, name="page%d" % t)
@@ -70,8 +85,8 @@ def tile_list_swab_cavity_scores_kernel(
             return page
 
         with tc.tile_pool(name="table", bufs=1) as table_pool:
-            scale_win = table_pool.tile([P, T], U8, name="scale_win")
-            nc.vector.memset(scale_win[:].bitcast(I32), 0)
+            scale_window = table_pool.tile([P, T], U8, name="scale_window")
+            nc.vector.memset(scale_window[:].bitcast(I32), 0)
             wb_planes = keep.tile([P, PASSES, H], U8, name="wb_planes", align_bytes=64)
             nc.vector.memset(wb_planes[:].bitcast(I32), 0)
             tab_planes = keep.tile([P, PASSES, S], U8, name="tab_planes", align_bytes=64)
@@ -82,25 +97,28 @@ def tile_list_swab_cavity_scores_kernel(
             wb_first = load_wb("wb_first", 0, 1)
             vector_rows = keep.tile([P, P], F32, name="vector_rows")
             nc.gpsimd.memset(vector_rows[:], 0.0)
+            scale_rows = PASSES * 4 * QUADRANTS
             nc.sync.dma_start(
-                scale_win[0:96:2, :].bitcast(I32), tab_scales.rearrange("a i t -> i a t").bitcast(I32)
+                scale_window[0 : 2 * scale_rows : 2, :].bitcast(I32),
+                tab_scales.rearrange("a q t -> q a t").bitcast(I32),
             )
             tabs = [load_table(0)]
-            for q in range(4):
+            for quad in range(QUADRANTS):
                 nc.sync.dma_start(
-                    wb_planes[32 * q : 32 * q + 4, :, :].bitcast(I32),
-                    wb_scales[:, 4 * q : 4 * q + 4, :].rearrange("a r n -> r a n").bitcast(I32),
+                    wb_planes[32 * quad : 32 * quad + 4, :, :].bitcast(I32),
+                    wb_scales[:, 4 * quad : 4 * quad + 4, :].rearrange("a r c -> r a c").bitcast(I32),
                 )
-            load_vector_rows(vector_rows, 0, gain)
-            load_vector_rows(vector_rows, 1, sx)
+            load_vector_rows(0, gain)
+            load_vector_rows(1, sx)
             tabs.append(load_table(1))
-            load_vector_rows(vector_rows, 2, sv)
+            load_vector_rows(2, sv)
             picked_scales = keep.tile([P, S], U8, name="picked_scales")
-            nc.vector.tensor_copy(picked_scales[:], scale_win[:].indirect(idx[:]))
-            for q in range(4):
+            nc.vector.tensor_copy(picked_scales[:], scale_window[:].indirect(idx[:]))
+            span = 2 * scale_rows // QUADRANTS
+            for quad in range(QUADRANTS):
                 nc.sync.dma_start(
-                    tab_planes[32 * q : 32 * q + 4, :, :].bitcast(I32),
-                    picked_scales[24 * q : 24 * q + 24 : 2, :].bitcast(I32),
+                    tab_planes[32 * quad : 32 * quad + 4, :, :].bitcast(I32),
+                    picked_scales[span * quad : span * (quad + 1) : 2, :].bitcast(I32),
                 )
             tabs.append(load_table(2))
             idx2 = load_list("idx2", offs2)
@@ -116,8 +134,8 @@ def tile_list_swab_cavity_scores_kernel(
             pages.append(load_page(1))
             wa_raw.append(load_wa(3))
             pages.append(load_page(2))
-            wr_raw = keep.tile([P, 4 * H], F32, name="wr_raw")
-            nc.sync.dma_start(wr_raw[:], wr.rearrange("(p j) n -> p (j n)", j=4))
+            wr_raw = keep.tile([P, PACK * H], F32, name="wr_raw")
+            nc.sync.dma_start(wr_raw[:], wr.rearrange("(p i) n -> p (i n)", i=PACK))
             pages.append(load_page(3))
 
             ident32 = keep.tile([P, P], F32, name="ident32")
@@ -136,58 +154,63 @@ def tile_list_swab_cavity_scores_kernel(
             for a in range(PASSES):
                 words = keep.tile([P, S], U32, name="picked%d" % a, align_bytes=64)
                 for h in range(2):
-                    half = words[:, HALF * h : HALF * (h + 1)]
-                    nc.vector.tensor_copy(half, tabs[a][:].bitcast(U32).indirect(idx[:, 32 * h : 32 * (h + 1)]))
+                    window = tabs[a][:].bitcast(U32).indirect(entries_of(idx, HALF * h, HALF))
+                    nc.vector.tensor_copy(words[:, HALF * h : HALF * (h + 1)], window)
                 picked.append(words)
 
         late = ctx.enter_context(tc.tile_pool(name="late", bufs=1))
 
-        SEAM = 1024
-        boards = [keep.tile([P, SEAM + 512], F32, name="board%d" % i, align_bytes=64) for i in range(TILES + 1)]
-        first_staging = keep.tile([P, PASSES * 512], BF16, name="first_staging", align_bytes=64)
+        boards = [keep.tile([P, SEAM + NP // 2], F32, name="board%d" % b, align_bytes=64) for b in range(TILES + 1)]
+        first_staging = keep.tile([P, WA_WIDTH], BF16, name="first_staging", align_bytes=64)
 
-        def left_of_seam(t, width):
-            return boards[t][:, SEAM - width // 2 : SEAM].bitcast(BF16)
+        def left_of_seam(board, width):
+            return boards[board][:, SEAM - width // 2 : SEAM].bitcast(BF16)
 
-        def right_of_seam(t, width):
-            return boards[t][:, SEAM : SEAM + width // 2].bitcast(BF16)
+        def right_of_seam(board, width):
+            return boards[board][:, SEAM : SEAM + width // 2].bitcast(BF16)
 
-        def quantize_wa(t, grouped):
-            nc.scalar.copy(
-                grouped.rearrange("p (a c i j) -> p a c j i", a=PASSES, i=4, j=4),
-                wa_raw[t][:].rearrange("p (a j c i) -> p a c j i", a=PASSES, i=4, j=4),
-            )
+        def on_seam(board, count):
+            return boards[board][:, SEAM + OVERLAP - count : SEAM + OVERLAP]
+
+        def quantize_wa(t, stagings):
+            share = PASSES // len(stagings)
+            for part, grouped in enumerate(stagings):
+                raw = wa_raw[t][:, K_PASS * share * part : K_PASS * share * (part + 1)]
+                nc.scalar.copy(
+                    grouped.rearrange("p (a c e i) -> p a c i e", a=share, e=4, i=PACK),
+                    raw.rearrange("p (a i c e) -> p a c i e", a=share, e=4, i=PACK),
+                )
             codes = keep.tile([P, PASSES * P], U32, name="wa_codes%d" % t, align_bytes=64)
             planes = keep.tile([P, PASSES * P], U8, name="wa_planes%d" % t, align_bytes=64)
             for a in range(PASSES):
                 nc.vector.quantize_mx(
                     out=codes[:, P * a : P * (a + 1)].bitcast(FP8X4),
                     scales=planes[:, P * a : P * (a + 1)],
-                    in_=grouped[:, 512 * a : 512 * (a + 1)],
+                    in_=stagings[a // share][:, K_PASS * (a % share) : K_PASS * (a % share + 1)],
                 )
             return codes, planes
 
         def quantize_wr(grouped):
             nc.scalar.copy(
-                grouped.rearrange("p (c i j) -> p c j i", i=4, j=4),
-                wr_raw[:].rearrange("p (j c i) -> p c j i", j=4, i=4),
+                grouped.rearrange("p (c e i) -> p c i e", e=4, i=PACK),
+                wr_raw[:].rearrange("p (i c e) -> p c i e", e=4, i=PACK),
             )
             codes = keep.tile([P, H], U32, name="wr_codes", align_bytes=64)
             plane = keep.tile([P, H], U8, name="wr_plane", align_bytes=64)
             nc.vector.quantize_mx(out=codes[:].bitcast(FP8X4), scales=plane[:], in_=grouped)
             return codes, plane
 
-        def open_sums(n):
-            if 2 * n <= HALF:
-                bank = psum.tile([P, 2 * n], F32, name="both", tag="mx")
-                return bank[:, 0:n], bank[:, n : 2 * n]
-            warm = psum.tile([P, n], F32, name="warm", tag="mx")
-            wear = psum.tile([P, n], F32, name="wear", tag="mx")
+        def open_sums(count):
+            if 2 * count <= HALF:
+                bank = psum.tile([P, 2 * count], F32, name="both", tag="mx")
+                return bank[:, 0:count], bank[:, count : 2 * count]
+            warm = psum.tile([P, count], F32, name="warm", tag="mx")
+            wear = psum.tile([P, count], F32, name="wear", tag="mx")
             return warm[:], wear[:]
 
-        def multiply(t, j0, n, sums, which, a):
-            shared = 2 * n <= HALF
-            if which == 0:
+        def multiply(t, j0, count, sums, which, a):
+            shared = 2 * count <= HALF
+            if which == WARM:
                 wa_codes, wa_planes = quantized[t]
                 rhs = wa_codes[:, P * a : P * (a + 1)].bitcast(FP8X4)
                 rhs_scale = wa_planes[:, P * a : P * (a + 1)]
@@ -195,154 +218,135 @@ def tile_list_swab_cavity_scores_kernel(
                 wb_codes = wb_first[:, a, :] if t == 0 else wb_rest[:, a, 2 * P * (t - 1) : 2 * P * t]
                 rhs = wb_codes.bitcast(FP4X4)
                 rhs_scale = wb_planes[:, a, P * t : P * (t + 1)]
-            blocks = n // P
-            for b in range(blocks):
+            for b in range(count // P):
                 cols = slice(j0 + P * b, j0 + P * (b + 1))
                 nc.tensor.matmul_mx(
                     out=sums[which][:, P * b : P * (b + 1)],
                     lhsT=picked[a][:, cols].bitcast(FP8X4), lhsT_scale=tab_planes[:, a, cols],
                     rhs=rhs, rhs_scale=rhs_scale,
-                    start=(a == 0 and b == 0 and not (shared and which == 1)),
-                    stop=(a == PASSES - 1 and b == blocks - 1 and not (shared and which == 0)),
+                    start=(a == 0 and b == 0 and not (shared and which == WEAR)),
+                    stop=(a == PASSES - 1 and b == count // P - 1 and not (shared and which == WARM)),
                 )
 
-        def first_stage(t, j0, n, magnitude, entries):
-            sums = open_sums(n)
-            for which in range(2):
-                for a in range(PASSES):
-                    multiply(t, j0, n, sums, which, a)
-            make_entries(t, n, sums, magnitude, entries)
-
-        def make_entries(t, n, sums, magnitude, entries):
-            warm, wear = sums
-            blocks = n // P
-            neg_tanh = ring.tile([P, n], F32, name="neg_tanh")
-            nc.scalar.activation(neg_tanh[:], warm, ACT.Tanh, scale=-1.0)
-            nc.scalar.activation(magnitude, wear, ACT.Abs)
-            turned = psum.tile([P, n], F32, name="turned", tag="tr")
-            for i, term in enumerate((neg_tanh[:], magnitude)):
-                for b in range(blocks):
+        def make_entries(t, count, sums, magnitude, entries):
+            neg_tanh = ring.tile([P, count], F32, name="neg_tanh")
+            nc.scalar.activation(neg_tanh[:], sums[WARM], ACT.Tanh, scale=-1.0)
+            nc.scalar.activation(magnitude, sums[WEAR], ACT.Abs)
+            turned = psum.tile([P, count], F32, name="turned", tag="tr")
+            for which, term in ((WARM, neg_tanh[:]), (WEAR, magnitude)):
+                for b in range(count // P):
                     cols = slice(P * b, P * (b + 1))
                     nc.tensor.matmul(
                         turned[:, cols], term[:, cols], ident32[:], is_transpose=True,
-                        start=(i == 0 and b == 0), stop=(i == 1 and b == blocks - 1),
+                        start=(which == WARM and b == 0), stop=(which == WEAR and b == count // P - 1),
                     )
             nc.scalar.activation(entries, turned[:], ACT.Copy, scale=neg_gain[:, t : t + 1])
+
+        def first_stage(t):
+            entries = ring.tile([P, S], F32, name="entries")
+            magnitude = ring.tile([P, HALF], F32, name="magnitude")
+            for h, target in enumerate((magnitude[:], on_seam(t, HALF))):
+                sums = open_sums(HALF)
+                for which in (WARM, WEAR):
+                    for a in range(PASSES):
+                        multiply(t, HALF * h, HALF, sums, which, a)
+                make_entries(t, HALF, sums, target, entries[:, HALF * h : HALF * (h + 1)])
+            return entries
 
         wide = late.tile([P, 2 * NP], F32, name="wide")
         narrow = late.tile([P, NP], F32, name="narrow")
         x_turned = [
-            flat.rearrange("p (b u q) -> p b u q", b=SUB, u=2) for flat in (narrow[:], wide[:, 64 : 64 + NP])
+            flat.rearrange("p (b u q) -> p b u q", b=BLOCKS, u=2)
+            for flat in (narrow[:], wide[:, OVERLAP : OVERLAP + NP])
         ]
-        sisters = {}
+        sisters, scaled = {}, {}
 
-        def gather_sister(t, dst):
-            nc.vector.tensor_copy(dst, pages[t][:].indirect(idx4[:]))
-            sisters[t] = dst
+        def gather_sister(t, target):
+            nc.vector.tensor_copy(target, pages[t][:].indirect(idx4[:]))
+            sisters[t] = target
 
-        scaled = {}
+        def scale_sister(t, target):
+            nc.scalar.activation(target, sisters[t], ACT.Copy, scale=sv_cols[:, t : t + 1])
+            scaled[t] = target
 
-        def scale_sister(t, dst):
-            nc.scalar.activation(dst, sisters[t], ACT.Copy, scale=sv_cols[:, t : t + 1])
-            scaled[t] = dst
-
-        def put(t, j0, n, entries):
-            nc.vector.tensor_tensor(
-                pages[t][:].indirect(idx2[:, j0 // 16 : (j0 + n) // 16]), entries, wgs_sb[:, j0 : j0 + n], ALU.mult
-            )
+        def put(t, j0, count, entries):
+            window = pages[t][:].indirect(entries_of(idx2, j0, count))
+            nc.vector.tensor_tensor(window, entries, wgs_sb[:, j0 : j0 + count], ALU.mult)
 
         def turn_x(t, x_rows, due, pieces):
-            n = NP // pieces
-            for i in range(pieces):
-                cols = slice(i * n, (i + 1) * n)
+            width = NP // pieces
+            for piece in range(pieces):
+                cols = slice(piece * width, (piece + 1) * width)
                 nc.scalar.activation(x_rows[:, cols], due[:, cols], ACT.Copy, scale=sx_cols[:, t : t + 1])
             for h in range(2):
-                x_cols = psum.tile([P, SUB, P], BF16, name="x_cols", tag="tr")
-                for b in range(SUB):
-                    c0 = HALF * h + P * b
-                    nc.tensor.transpose(x_cols[:, b, :], x_rows[:, c0 : c0 + P], ident16[:])
+                x_cols = psum.tile([P, BLOCKS, P], BF16, name="x_cols", tag="tr")
+                for b in range(BLOCKS):
+                    j0 = HALF * h + P * b
+                    nc.tensor.transpose(x_cols[:, b, :], x_rows[:, j0 : j0 + P], ident16[:])
                 nc.scalar.copy(
                     x_turned[h][:, :, :, 32 * t : 32 * (t + 1)],
                     x_cols[:].bitcast(F32).rearrange("p b (q u) -> p b u q", u=2),
                 )
 
-        def on_seam(i, n=HALF):
-            return boards[i][:, SEAM + 64 - n : SEAM + 64]
-
-        def both_halves(t):
-            entries = ring.tile([P, S], F32, name="entries")
-            magnitude = ring.tile([P, HALF], F32, name="magnitude")
-            first_stage(t, 0, HALF, magnitude[:], entries[:, 0:HALF])
-            first_stage(t, HALF, HALF, on_seam(t), entries[:, HALF:S])
-            return entries
-
-        WA_WIDTH = PASSES * 512
-        quantized = [quantize_wa(0, first_staging[:])]
+        quantized = [quantize_wa(0, [first_staging[:]])]
         opening = ring.tile([P, S], F32, name="entries")
-        QUARTER = HALF // 2
         spans = [(0, QUARTER), (QUARTER, QUARTER), (HALF, HALF)]
-        opening_sums = [open_sums(n) for j0, n in spans]
+        opening_sums = [open_sums(count) for j0, count in spans]
         for a in range(PASSES):
-            for (j0, n), sums in zip(spans, opening_sums):
-                for which in range(2):
-                    multiply(0, j0, n, sums, which, a)
+            for (j0, count), sums in zip(spans, opening_sums):
+                for which in (WARM, WEAR):
+                    multiply(0, j0, count, sums, which, a)
         first_magnitude = ring.tile([P, QUARTER], F32, name="magnitude")
         make_entries(0, QUARTER, opening_sums[0], first_magnitude[:], opening[:, 0:QUARTER])
         make_entries(0, QUARTER, opening_sums[1], on_seam(TILES, QUARTER), opening[:, QUARTER:HALF])
-        quantized.append(quantize_wa(1, left_of_seam(TILES, WA_WIDTH)))
-        second_half = wa_raw[1][:, 2 * HALF : 3 * HALF]
-        make_entries(0, HALF, opening_sums[2], on_seam(0), second_half)
-        parts = [(0, QUARTER, opening[:, 0:QUARTER]), (QUARTER, QUARTER, opening[:, QUARTER:HALF]), (HALF, HALF, second_half)]
+        third_staging = wa_raw[1][:, 0 : K_PASS // 2].bitcast(BF16)
+        quantized.append(quantize_wa(1, [left_of_seam(TILES, K_PASS), right_of_seam(TILES, K_PASS), third_staging]))
+        second_half = wa_raw[1][:, 2 * K_PASS : 3 * K_PASS]
+        make_entries(0, HALF, opening_sums[2], on_seam(0, HALF), second_half)
+        parts = [
+            (0, QUARTER, opening[:, 0:QUARTER]), (QUARTER, QUARTER, opening[:, QUARTER:HALF]), (HALF, HALF, second_half),
+        ]
         last_rows = late.tile([P, NP], BF16, name="last_rows")
         first_sister = late.tile([P, NP], F32, name="first_sister")
+        due_tiles = [wa_raw[0], wa_raw[3], wa_raw[2], wa_raw[1]]
         for t in range(TILES):
             for part in parts:
                 put(t, *part)
-            if t == 0:
-                quantized.append(quantize_wa(2, left_of_seam(0, WA_WIDTH)))
-            elif t == 1:
-                quantized.append(quantize_wa(3, left_of_seam(1, WA_WIDTH)))
-            due = (wa_raw[0], wa_raw[3], wr_raw, wa_raw[1])[t][:, 0:NP]
-            pieces = 2 if t == TILES - 1 else 1
-            for i in range(pieces):
-                n = NP // pieces
-                nc.vector.tensor_copy(
-                    due[:, i * n : (i + 1) * n], pages[t][:].indirect(idx3[:, i * n // 16 : (i + 1) * n // 16])
-                )
+            if t + 2 < TILES:
+                quantized.append(quantize_wa(t + 2, [left_of_seam(t, WA_WIDTH)]))
+            due = due_tiles[t][:, 0:NP]
+            pieces = 2 if t == LAST else 1
+            width = NP // pieces
+            for piece in range(pieces):
+                window = pages[t][:].indirect(entries_of(idx3, piece * width, width))
+                nc.vector.tensor_copy(due[:, piece * width : (piece + 1) * width], window)
             if t == 0:
                 gather_sister(0, first_sister[:])
-            if t + 1 < TILES:
-                entries = both_halves(t + 1)
-                if t == 0:
-                    parts = [(0, HALF, entries[:, 0:HALF]), (HALF, HALF, entries[:, HALF:S])]
-                else:
-                    parts = [(0, S, entries[:])]
-                if t == 1:
-                    wr_codes, wr_plane = quantize_wr(left_of_seam(2, 4 * H))
+            if t < LAST:
+                entries = first_stage(t + 1)
+                parts = [(0, HALF, entries[:, 0:HALF]), (HALF, HALF, entries[:, HALF:S])]
                 turn_x(t, right_of_seam(t + 1, NP), due, pieces)
             else:
                 turn_x(t, last_rows[:], due, pieces)
-            if t == 0:
+            if t == LAST - 1:
+                wr_codes, wr_plane = quantize_wr(left_of_seam(LAST, PACK * H))
                 scale_sister(0, due)
         gather_sister(1, wgs_sb[:])
         gather_sister(2, entries[:])
 
-        x_grouped, x_codes, x_planes = [], [], []
+        x_codes, x_planes = [], []
         for h in range(2):
-            grouped = late.tile([P, 4 * HALF], BF16, name="x_grouped%d" % h, align_bytes=64)
-            for g in range(2):
+            grouped = late.tile([P, PACK * HALF], BF16, name="x_grouped%d" % h, align_bytes=64)
+            for bank in range(BLOCKS // 2):
                 back = psum.tile([P, 2, 2, P], F32, name="back", tag="tr")
                 for b in range(2):
                     for u in range(2):
-                        nc.tensor.transpose(back[:, b, u, :], x_turned[h][:, 2 * g + b, u, :], ident32[:])
-                nc.scalar.copy(
-                    grouped[:].bitcast(F32)[:, 512 * g : 512 * (g + 1)].rearrange("p (b j u) -> p b j u", b=2, u=2),
-                    back[:].rearrange("p b u j -> p b j u"),
-                )
+                        nc.tensor.transpose(back[:, b, u, :], x_turned[h][:, 2 * bank + b, u, :], ident32[:])
+                pairs = grouped[:].bitcast(F32)[:, HALF * bank : HALF * (bank + 1)]
+                nc.scalar.copy(pairs.rearrange("p (b j u) -> p b j u", b=2, u=2), back[:].rearrange("p b u j -> p b j u"))
             codes = late.tile([P, HALF], U32, name="x_codes%d" % h, align_bytes=64)
             plane = late.tile([P, HALF], U8, name="x_plane%d" % h, align_bytes=64)
             nc.vector.quantize_mx(out=codes[:].bitcast(FP8X4), scales=plane[:], in_=grouped[:])
-            x_grouped.append(grouped)
             x_codes.append(codes)
             x_planes.append(plane)
         scale_sister(1, wide[:, 0:NP])
@@ -350,32 +354,37 @@ def tile_list_swab_cavity_scores_kernel(
 
         def take_min(t, h):
             y = psum.tile([P, HALF], F32, name="y", tag="mx")
+            rows = slice(P * t, P * (t + 1))
             nc.tensor.matmul_mx(
-                out=y[:], lhsT=wr_codes[:, P * t : P * (t + 1)].bitcast(FP8X4), lhsT_scale=wr_plane[:, P * t : P * (t + 1)],
+                out=y[:], lhsT=wr_codes[:, rows].bitcast(FP8X4), lhsT_scale=wr_plane[:, rows],
                 rhs=x_codes[h][:].bitcast(FP8X4), rhs_scale=x_planes[h][:], start=True, stop=True,
             )
             lesser = late.tile([P, HALF], F32, name="lesser%d_%d" % (t, h))
-            nc.vector.scalar_tensor_tensor(
-                lesser[:], sisters[t][:, HALF * h : HALF * (h + 1)], sv_cols[:, t : t + 1], y[:], ALU.mult, ALU.min
-            )
+            cols = slice(HALF * h, HALF * (h + 1))
+            if t < LAST:
+                nc.vector.tensor_tensor(lesser[:], scaled[t][:, cols], y[:], ALU.min)
+            else:
+                nc.vector.scalar_tensor_tensor(
+                    lesser[:], sisters[t][:, cols], sv_cols[:, t : t + 1], y[:], ALU.mult, ALU.min
+                )
             return lesser
 
-        def add_and_store(t, h, lesser, engine):
+        def add_and_store(t, h, lesser):
             cols = slice(HALF * h, HALF * (h + 1))
-            result = late.tile([P, HALF], F32, name="result", bufs=4)
-            if t in scaled:
-                engine.tensor_tensor(result[:], lesser[:], scaled[t][:, cols], ALU.add)
+            result = late.tile([P, HALF], F32, name="result%d_%d" % (t, h))
+            if t < LAST:
+                nc.gpsimd.tensor_tensor(result[:], lesser[:], scaled[t][:, cols], ALU.add)
             else:
-                engine.scalar_tensor_tensor(
+                nc.vector.scalar_tensor_tensor(
                     result[:], sisters[t][:, cols], sv_cols[:, t : t + 1], lesser[:], ALU.mult, ALU.add
                 )
             nc.sync.dma_start(out[P * t : P * (t + 1), cols], result[:])
 
+        for group in ((0, 1), (2,)):
+            for h in range(2):
+                for t in group:
+                    add_and_store(t, h, take_min(t, h))
+        gather_sister(LAST, sisters[LAST - 1])
+        lessers = [take_min(LAST, h) for h in range(2)]
         for h in range(2):
-            for t in range(TILES - 1):
-                add_and_store(t, h, take_min(t, h), nc.gpsimd)
-        last = TILES - 1
-        gather_sister(last, sisters[last - 1])
-        lessers = [take_min(last, h) for h in range(2)]
-        for h in range(2):
-            add_and_store(last, h, lessers[h], nc.vector)
+            add_and_store(LAST, h, lessers[h])

from contextlib import ExitStack

import concourse.mybir as mybir
from concourse.masks import make_identity

K, H, T, S, T2, NP = 1536, 512, 4096, 1024, 2048, 1024
FLOPS = 2 * K * H * S * 2 + 2 * H * H * NP

F32 = mybir.dt.float32
BF16 = mybir.dt.bfloat16
I32 = mybir.dt.int32
U32 = mybir.dt.uint32
U16 = mybir.dt.uint16
U8 = mybir.dt.uint8
FP8X4 = mybir.dt.float8_e4m3fn_x4
FP4X4 = mybir.dt.float4_e2m1fn_x4
ALU = mybir.AluOpType
ACT = mybir.ActivationFunctionType

P = 128
PACK = 4
K_PASS = P * PACK
PASSES = K // K_PASS
TILES = H // P
LAST = TILES - 1
QUADRANTS = 4
LIST_ROWS = 16
HALF = 512
QUARTER = HALF // 2
BLOCKS = HALF // P
WA_WIDTH = PASSES * K_PASS
WARM, WEAR = 0, 1
SEAM = 1024
OVERLAP = P // 2


def tile_list_swab_cavity_scores_kernel(
    tc, tab_words, tab_scales, offs, offs2, offs3, offs4, wa, wb_words, wb_scales,
    gain, wgs, page0, sx, wr, sv, out,
):
    nc = tc.nc
    with ExitStack() as ctx:
        keep = ctx.enter_context(tc.tile_pool(name="keep", bufs=1))
        ring = ctx.enter_context(tc.tile_pool(name="ring", bufs=2))
        psum = ctx.enter_context(tc.psum_pool(name="psum", bufs=4))

        def entries_of(offsets, j0, count):
            return offsets[:, j0 // LIST_ROWS : (j0 + count) // LIST_ROWS]

        def load_list(name, source):
            offsets = keep.tile([P, S // LIST_ROWS], U16, name=name)
            nc.sync.dma_start(offsets[:], source)
            return offsets

        def load_table(a):
            tab = table_pool.tile([P, T], I32, name="tab%d" % a)
            nc.sync.dma_start(tab[:], tab_words[a].rearrange("p t i -> p (t i)").bitcast(I32))
            return tab

        def load_wa(t):
            raw = keep.tile([P, WA_WIDTH], F32, name="wa_raw%d" % t, align_bytes=64)
            for a in range(PASSES):
                rows = slice(K_PASS * a, K_PASS * (a + 1))
                nc.sync.dma_start(
                    raw[:, rows].rearrange("p (i c) -> p i c", i=PACK),
                    wa[rows, P * t : P * (t + 1)].rearrange("(p i) c -> p i c", i=PACK),
                )
            return raw

        def load_wb(name, t0, t1):
            codes = keep.tile([P, PASSES, 2 * P * (t1 - t0)], U8, name=name, align_bytes=64)
            nc.sync.dma_start(
                codes[:].bitcast(I32),
                wb_words[:, :, 2 * P * t0 : 2 * P * t1].rearrange("a p c -> p a c").bitcast(I32),
            )
            return codes

        def load_vector_rows(place, vector):
            rows = vector_rows[TILES * place : TILES * (place + 1), :]
            nc.sync.dma_start(rows, vector.rearrange("(t p) -> t p", p=P))

        def load_page(t):
            page = keep.tile([P, T2], F32, name="page%d" % t)
            nc.sync.dma_start(page[:], page0[P * t : P * (t + 1), :])
            return page

        with tc.tile_pool(name="table", bufs=1) as table_pool:
            scale_window = table_pool.tile([P, T], U8, name="scale_window")
            nc.vector.memset(scale_window[:].bitcast(I32), 0)
            wb_planes = keep.tile([P, PASSES, H], U8, name="wb_planes", align_bytes=64)
            nc.vector.memset(wb_planes[:].bitcast(I32), 0)
            tab_planes = keep.tile([P, PASSES, S], U8, name="tab_planes", align_bytes=64)
            nc.vector.memset(tab_planes[:].bitcast(I32), 0)

            idx = load_list("idx", offs)
            wa_raw = [load_wa(0)]
            wb_first = load_wb("wb_first", 0, 1)
            vector_rows = keep.tile([P, P], F32, name="vector_rows")
            nc.gpsimd.memset(vector_rows[:], 0.0)
            scale_rows = PASSES * 4 * QUADRANTS
            nc.sync.dma_start(
                scale_window[0 : 2 * scale_rows : 2, :].bitcast(I32),
                tab_scales.rearrange("a q t -> q a t").bitcast(I32),
            )
            tabs = [load_table(0)]
            for quad in range(QUADRANTS):
                nc.sync.dma_start(
                    wb_planes[32 * quad : 32 * quad + 4, :, :].bitcast(I32),
                    wb_scales[:, 4 * quad : 4 * quad + 4, :].rearrange("a r c -> r a c").bitcast(I32),
                )
            load_vector_rows(0, gain)
            load_vector_rows(1, sx)
            tabs.append(load_table(1))
            load_vector_rows(2, sv)
            picked_scales = keep.tile([P, S], U8, name="picked_scales")
            nc.vector.tensor_copy(picked_scales[:], scale_window[:].indirect(idx[:]))
            span = 2 * scale_rows // QUADRANTS
            for quad in range(QUADRANTS):
                nc.sync.dma_start(
                    tab_planes[32 * quad : 32 * quad + 4, :, :].bitcast(I32),
                    picked_scales[span * quad : span * (quad + 1) : 2, :].bitcast(I32),
                )
            tabs.append(load_table(2))
            idx2 = load_list("idx2", offs2)
            pages = [load_page(0)]
            wgs_sb = keep.tile([P, S], F32, name="wgs_sb")
            nc.sync.dma_start(wgs_sb[:, 0:HALF], wgs[:, 0:HALF])
            wa_raw.append(load_wa(1))
            nc.sync.dma_start(wgs_sb[:, HALF:S], wgs[:, HALF:S])
            wb_rest = load_wb("wb_rest", 1, TILES)
            idx3 = load_list("idx3", offs3)
            idx4 = load_list("idx4", offs4)
            wa_raw.append(load_wa(2))
            pages.append(load_page(1))
            wa_raw.append(load_wa(3))
            pages.append(load_page(2))
            wr_raw = keep.tile([P, PACK * H], F32, name="wr_raw")
            nc.sync.dma_start(wr_raw[:], wr.rearrange("(p i) n -> p (i n)", i=PACK))
            pages.append(load_page(3))

            ident32 = keep.tile([P, P], F32, name="ident32")
            make_identity(nc, ident32[:])
            ident16 = keep.tile([P, P], BF16, name="ident16")
            make_identity(nc, ident16[:])
            vector_cols = psum.tile([P, P], F32, name="vector_cols", tag="tr")
            nc.tensor.transpose(vector_cols[:], vector_rows[:], ident32[:])
            neg_gain = keep.tile([P, TILES], F32, name="neg_gain")
            nc.vector.tensor_scalar(neg_gain[:], vector_cols[:, 0:TILES], -1.0, None, ALU.mult)
            factors = keep.tile([P, 2 * TILES], F32, name="factors")
            nc.vector.tensor_copy(factors[:], vector_cols[:, TILES : 3 * TILES])
            sx_cols, sv_cols = factors[:, 0:TILES], factors[:, TILES : 2 * TILES]

            picked = []
            for a in range(PASSES):
                words = keep.tile([P, S], U32, name="picked%d" % a, align_bytes=64)
                for h in range(2):
                    window = tabs[a][:].bitcast(U32).indirect(entries_of(idx, HALF * h, HALF))
                    nc.vector.tensor_copy(words[:, HALF * h : HALF * (h + 1)], window)
                picked.append(words)

        late = ctx.enter_context(tc.tile_pool(name="late", bufs=1))

        boards = [keep.tile([P, SEAM + NP // 2], F32, name="board%d" % b, align_bytes=64) for b in range(TILES + 1)]
        first_staging = keep.tile([P, WA_WIDTH], BF16, name="first_staging", align_bytes=64)

        def left_of_seam(board, width):
            return boards[board][:, SEAM - width // 2 : SEAM].bitcast(BF16)

        def right_of_seam(board, width):
            return boards[board][:, SEAM : SEAM + width // 2].bitcast(BF16)

        def on_seam(board, count):
            return boards[board][:, SEAM + OVERLAP - count : SEAM + OVERLAP]

        def quantize_wa(t, stagings):
            share = PASSES // len(stagings)
            for part, grouped in enumerate(stagings):
                raw = wa_raw[t][:, K_PASS * share * part : K_PASS * share * (part + 1)]
                nc.scalar.copy(
                    grouped.rearrange("p (a c e i) -> p a c i e", a=share, e=4, i=PACK),
                    raw.rearrange("p (a i c e) -> p a c i e", a=share, e=4, i=PACK),
                )
            codes = keep.tile([P, PASSES * P], U32, name="wa_codes%d" % t, align_bytes=64)
            planes = keep.tile([P, PASSES * P], U8, name="wa_planes%d" % t, align_bytes=64)
            for a in range(PASSES):
                nc.vector.quantize_mx(
                    out=codes[:, P * a : P * (a + 1)].bitcast(FP8X4),
                    scales=planes[:, P * a : P * (a + 1)],
                    in_=stagings[a // share][:, K_PASS * (a % share) : K_PASS * (a % share + 1)],
                )
            return codes, planes

        def quantize_wr(grouped):
            nc.scalar.copy(
                grouped.rearrange("p (c e i) -> p c i e", e=4, i=PACK),
                wr_raw[:].rearrange("p (i c e) -> p c i e", e=4, i=PACK),
            )
            codes = keep.tile([P, H], U32, name="wr_codes", align_bytes=64)
            plane = keep.tile([P, H], U8, name="wr_plane", align_bytes=64)
            nc.vector.quantize_mx(out=codes[:].bitcast(FP8X4), scales=plane[:], in_=grouped)
            return codes, plane

        def open_sums(count):
            if 2 * count <= HALF:
                bank = psum.tile([P, 2 * count], F32, name="both", tag="mx")
                return bank[:, 0:count], bank[:, count : 2 * count]
            warm = psum.tile([P, count], F32, name="warm", tag="mx")
            wear = psum.tile([P, count], F32, name="wear", tag="mx")
            return warm[:], wear[:]

        def multiply(t, j0, count, sums, which, a):
            shared = 2 * count <= HALF
            if which == WARM:
                wa_codes, wa_planes = quantized[t]
                rhs = wa_codes[:, P * a : P * (a + 1)].bitcast(FP8X4)
                rhs_scale = wa_planes[:, P * a : P * (a + 1)]
            else:
                wb_codes = wb_first[:, a, :] if t == 0 else wb_rest[:, a, 2 * P * (t - 1) : 2 * P * t]
                rhs = wb_codes.bitcast(FP4X4)
                rhs_scale = wb_planes[:, a, P * t : P * (t + 1)]
            for b in range(count // P):
                cols = slice(j0 + P * b, j0 + P * (b + 1))
                nc.tensor.matmul_mx(
                    out=sums[which][:, P * b : P * (b + 1)],
                    lhsT=picked[a][:, cols].bitcast(FP8X4), lhsT_scale=tab_planes[:, a, cols],
                    rhs=rhs, rhs_scale=rhs_scale,
                    start=(a == 0 and b == 0 and not (shared and which == WEAR)),
                    stop=(a == PASSES - 1 and b == count // P - 1 and not (shared and which == WARM)),
                )

        def make_entries(t, count, sums, magnitude, entries):
            neg_tanh = ring.tile([P, count], F32, name="neg_tanh")
            nc.scalar.activation(neg_tanh[:], sums[WARM], ACT.Tanh, scale=-1.0)
            nc.scalar.activation(magnitude, sums[WEAR], ACT.Abs)
            turned = psum.tile([P, count], F32, name="turned", tag="tr")
            for which, term in ((WARM, neg_tanh[:]), (WEAR, magnitude)):
                for b in range(count // P):
                    cols = slice(P * b, P * (b + 1))
                    nc.tensor.matmul(
                        turned[:, cols], term[:, cols], ident32[:], is_transpose=True,
                        start=(which == WARM and b == 0), stop=(which == WEAR and b == count // P - 1),
                    )
            nc.scalar.activation(entries, turned[:], ACT.Copy, scale=neg_gain[:, t : t + 1])

        def first_stage(t):
            entries = ring.tile([P, S], F32, name="entries")
            magnitude = ring.tile([P, HALF], F32, name="magnitude")
            for h, target in enumerate((magnitude[:], on_seam(t, HALF))):
                sums = open_sums(HALF)
                for which in (WARM, WEAR):
                    for a in range(PASSES):
                        multiply(t, HALF * h, HALF, sums, which, a)
                make_entries(t, HALF, sums, target, entries[:, HALF * h : HALF * (h + 1)])
            return entries

        wide = late.tile([P, 2 * NP], F32, name="wide")
        narrow = late.tile([P, NP], F32, name="narrow")
        x_turned = [
            flat.rearrange("p (b u q) -> p b u q", b=BLOCKS, u=2)
            for flat in (narrow[:], wide[:, OVERLAP : OVERLAP + NP])
        ]
        sisters, scaled = {}, {}

        def gather_sister(t, target):
            nc.vector.tensor_copy(target, pages[t][:].indirect(idx4[:]))
            sisters[t] = target

        def scale_sister(t, target):
            nc.scalar.activation(target, sisters[t], ACT.Copy, scale=sv_cols[:, t : t + 1])
            scaled[t] = target

        def put(t, j0, count, entries):
            window = pages[t][:].indirect(entries_of(idx2, j0, count))
            nc.vector.tensor_tensor(window, entries, wgs_sb[:, j0 : j0 + count], ALU.mult)

        def turn_x(t, x_rows, due, pieces):
            width = NP // pieces
            for piece in range(pieces):
                cols = slice(piece * width, (piece + 1) * width)
                nc.scalar.activation(x_rows[:, cols], due[:, cols], ACT.Copy, scale=sx_cols[:, t : t + 1])
            for h in range(2):
                x_cols = psum.tile([P, BLOCKS, P], BF16, name="x_cols", tag="tr")
                for b in range(BLOCKS):
                    j0 = HALF * h + P * b
                    nc.tensor.transpose(x_cols[:, b, :], x_rows[:, j0 : j0 + P], ident16[:])
                nc.scalar.copy(
                    x_turned[h][:, :, :, 32 * t : 32 * (t + 1)],
                    x_cols[:].bitcast(F32).rearrange("p b (q u) -> p b u q", u=2),
                )

        quantized = [quantize_wa(0, [first_staging[:]])]
        opening = ring.tile([P, S], F32, name="entries")
        spans = [(0, QUARTER), (QUARTER, QUARTER), (HALF, HALF)]
        opening_sums = [open_sums(count) for j0, count in spans]
        for a in range(PASSES):
            for (j0, count), sums in zip(spans, opening_sums):
                for which in (WARM, WEAR):
                    multiply(0, j0, count, sums, which, a)
        first_magnitude = ring.tile([P, QUARTER], F32, name="magnitude")
        make_entries(0, QUARTER, opening_sums[0], first_magnitude[:], opening[:, 0:QUARTER])
        make_entries(0, QUARTER, opening_sums[1], on_seam(TILES, QUARTER), opening[:, QUARTER:HALF])
        third_staging = wa_raw[1][:, 0 : K_PASS // 2].bitcast(BF16)
        quantized.append(quantize_wa(1, [left_of_seam(TILES, K_PASS), right_of_seam(TILES, K_PASS), third_staging]))
        second_half = wa_raw[1][:, 2 * K_PASS : 3 * K_PASS]
        make_entries(0, HALF, opening_sums[2], on_seam(0, HALF), second_half)
        parts = [
            (0, QUARTER, opening[:, 0:QUARTER]), (QUARTER, QUARTER, opening[:, QUARTER:HALF]), (HALF, HALF, second_half),
        ]
        last_rows = late.tile([P, NP], BF16, name="last_rows")
        first_sister = late.tile([P, NP], F32, name="first_sister")
        due_tiles = [wa_raw[0], wa_raw[3], wa_raw[2], wa_raw[1]]
        for t in range(TILES):
            for part in parts:
                put(t, *part)
            if t + 2 < TILES:
                quantized.append(quantize_wa(t + 2, [left_of_seam(t, WA_WIDTH)]))
            due = due_tiles[t][:, 0:NP]
            pieces = 2 if t == LAST else 1
            width = NP // pieces
            for piece in range(pieces):
                window = pages[t][:].indirect(entries_of(idx3, piece * width, width))
                nc.vector.tensor_copy(due[:, piece * width : (piece + 1) * width], window)
            if t == 0:
                gather_sister(0, first_sister[:])
            if t < LAST:
                entries = first_stage(t + 1)
                parts = [(0, HALF, entries[:, 0:HALF]), (HALF, HALF, entries[:, HALF:S])]
                turn_x(t, right_of_seam(t + 1, NP), due, pieces)
            else:
                turn_x(t, last_rows[:], due, pieces)
            if t == LAST - 1:
                wr_codes, wr_plane = quantize_wr(left_of_seam(LAST, PACK * H))
                scale_sister(0, due)
        gather_sister(1, wgs_sb[:])
        gather_sister(2, entries[:])

        x_codes, x_planes = [], []
        for h in range(2):
            grouped = late.tile([P, PACK * HALF], BF16, name="x_grouped%d" % h, align_bytes=64)
            for bank in range(BLOCKS // 2):
                back = psum.tile([P, 2, 2, P], F32, name="back", tag="tr")
                for b in range(2):
                    for u in range(2):
                        nc.tensor.transpose(back[:, b, u, :], x_turned[h][:, 2 * bank + b, u, :], ident32[:])
                pairs = grouped[:].bitcast(F32)[:, HALF * bank : HALF * (bank + 1)]
                nc.scalar.copy(pairs.rearrange("p (b j u) -> p b j u", b=2, u=2), back[:].rearrange("p b u j -> p b j u"))
            codes = late.tile([P, HALF], U32, name="x_codes%d" % h, align_bytes=64)
            plane = late.tile([P, HALF], U8, name="x_plane%d" % h, align_bytes=64)
            nc.vector.quantize_mx(out=codes[:].bitcast(FP8X4), scales=plane[:], in_=grouped[:])
            x_codes.append(codes)
            x_planes.append(plane)
        scale_sister(1, wide[:, 0:NP])
        scale_sister(2, wide[:, NP : 2 * NP])

        def take_min(t, h):
            y = psum.tile([P, HALF], F32, name="y", tag="mx")
            rows = slice(P * t, P * (t + 1))
            nc.tensor.matmul_mx(
                out=y[:], lhsT=wr_codes[:, rows].bitcast(FP8X4), lhsT_scale=wr_plane[:, rows],
                rhs=x_codes[h][:].bitcast(FP8X4), rhs_scale=x_planes[h][:], start=True, stop=True,
            )
            lesser = late.tile([P, HALF], F32, name="lesser%d_%d" % (t, h))
            cols = slice(HALF * h, HALF * (h + 1))
            if t < LAST:
                nc.vector.tensor_tensor(lesser[:], scaled[t][:, cols], y[:], ALU.min)
            else:
                nc.vector.scalar_tensor_tensor(
                    lesser[:], sisters[t][:, cols], sv_cols[:, t : t + 1], y[:], ALU.mult, ALU.min
                )
            return lesser

        def add_and_store(t, h, lesser):
            cols = slice(HALF * h, HALF * (h + 1))
            result = late.tile([P, HALF], F32, name="result%d_%d" % (t, h))
            if t < LAST:
                nc.gpsimd.tensor_tensor(result[:], lesser[:], scaled[t][:, cols], ALU.add)
            else:
                nc.vector.scalar_tensor_tensor(
                    result[:], sisters[t][:, cols], sv_cols[:, t : t + 1], lesser[:], ALU.mult, ALU.add
                )
            nc.sync.dma_start(out[P * t : P * (t + 1), cols], result[:])

        for group in ((0, 1), (2,)):
            for h in range(2):
                for t in group:
                    add_and_store(t, h, take_min(t, h))
        gather_sister(LAST, sisters[LAST - 1])
        lessers = [take_min(LAST, h) for h in range(2)]
        for h in range(2):
            add_and_store(LAST, h, lessers[h])
